import numpy as np, ml_dtypes
CORES = [2,6,10,14,18,22,26,30]
N = 8
BF = ml_dtypes.bfloat16
V, G, W, CAP, QA, QB, RO = 1024, 512, 2048, 96, 4, 4, 4
def deal(rng, a):
    return np.stack([rng.permutation(np.resize(np.array(a), 8)) for q in range(N)])
def parts(rng):
    sh = (N, 8, 16, V)
    mid = rng.integers(20, 236, (N, 8, 16, 16)); kin = rng.integers(0, 16, (N, 8, 1, V))
    x = np.take_along_axis(mid, kin, 3) + rng.integers(-20, 21, sh)
    low = deal(rng, [0.003, 0.01, 0.03])[:, :, None, None]; flat = deal(rng, [0, 1])[:, :, None, None] == 1
    r = np.where(flat, 255, rng.integers(130, 256, sh)); r = np.where(rng.random(sh) < low, rng.integers(1, 130, sh), r)
    p = np.where(rng.random(sh) < 0.15, rng.integers(1, 130, sh), 0)
    keep = deal(rng, [0.4, 0.7, 0.9])[:, :, None, None]
    s = np.where(rng.random(sh) < keep, np.arange(V), rng.integers(0, W, sh))
    c = np.where(rng.random(sh) < 0.5, rng.integers(0, V, sh), rng.integers(0, W, sh))
    h = deal(rng, [180, 230, 500, 1000, 1200]) + rng.integers(0, 32, (N, 8))
    return x, r, p, c, s, h
def pack(x, r, p, c, s, h):
    v = {"x": x, "reach": r, "past": p}
    d = {k: np.ascontiguousarray(v[k].reshape(N, 128, V)).astype(np.float32).astype(BF) for k in v}
    d["cand"] = np.ascontiguousarray(c.reshape(N, 128, V)).astype(np.int32); d["succ"] = np.ascontiguousarray(s.reshape(N, 128, V)).astype(np.int32)
    d["th"] = h.reshape(N, 8, 1).astype(np.int32)
    return d
def setup_inputs(rng):
    return pack(*parts(rng))
def setup_inputs_ends(rng):
    sh = (N, 8, 16, V); one = (N, 8, 1, V)
    x = 255 * np.where(rng.random(one) < 0.7, rng.integers(0, 2, one), rng.integers(0, 2, sh))
    x = np.where((rng.random(one) < 0.2) & (rng.random(sh) < 0.3), x + np.where(x == 0, 1, -1), x)
    k = rng.random(one); r = np.where(k < 0.5, 255, np.where(k < 0.6, 1, np.where(rng.random(sh) < 0.5, 1, 255)))
    p = 255 * ((rng.random(one) < 0.25) & (rng.random(sh) < 0.2)).astype(np.int64)
    c = np.where(rng.random(sh) < 0.65, (W - 1) * rng.integers(0, 2, sh), rng.integers(0, W, sh))
    s = np.where((rng.random(one) < 0.5) | (rng.random(sh) < 0.65), (W - 1) * rng.integers(0, 2, sh), rng.integers(0, W, sh))
    h = 4095 * rng.integers(0, 2, (N, 8)); h[:, 0] = 0; h[:, 4] = 4095; h[:, 7] = 4095
    for a in (0, 1, V - QA, V - 1, G - 1): p[..., a] = 0; r[..., a] = 255
    p[..., 2] = 255; r[..., 2] = 1; x[..., 0] = 0; x[..., V - QA] = 0
    for a in (1, V - 1): x[:, 1::2, :, a] = 255; x[:, ::2, :, a] = 0
    c[..., 0] = 2; c[:, :, 15, 0] = V - 1
    c[..., V - QA] = 2; c[:, :, 14, V - QA] = V - 1; c[:, :, 15, V - QA] = 1
    s[..., 0] = 0; s[..., G - 1] = W - 1
    return pack(x, r, p, c, s, h)
def setup_inputs_corners(rng):
    x, r, p, c, s, h = parts(rng); act = np.arange(0, G, QB); here = np.arange(V); ptr = np.array([0, V - 1, V, V + G - 1, V + G, W - 1])
    for q in range(N):
        for g in range(8):
            k = (g + q) % 8
            if k < 6:
                n = (0, 1, CAP - 1, CAP, CAP + 1, len(act))[k]; a = rng.permutation(act)[:n]
                h[q, g] = 0; x[q, g] = x[q, g][:, rng.integers(0, 16, V)]; r[q, g] = 200; r[q, g, :, V - 1] = 5
                p[q, g] = np.where(rng.random((16, V)) < 0.05, 10, 0)
                w = np.tile(here, (16, 1)); w[rng.integers(0, 16, n), a] = V - 1; s[q, g] = w
            elif k == 6:
                h[q, g] = 4095; p[q, g] = 0; c[q, g] = here - here % QA + (here + QA - 1) % QA
            else:
                h[q, g] = 4095; full = rng.random(V) < 0.5; full[0] = True; full[V - 1] = False; m = rng.random(V) < 0.5; n = int(np.count_nonzero(m))
                w = p[q, g].copy(); w[:, full] = 255; p[q, g] = w
                w = np.where(rng.random((16, V)) < 0.5, rng.integers(V, W, (16, V)), (here + QA * rng.integers(0, V // QA, (16, V))) % V)
                w[:, m] = rng.choice(here[full], (16, n)); w[15, m] = rng.integers(0, V, n); c[q, g] = w
                s[q, g] = np.where(rng.random((16, V)) < 0.3, here, ptr[rng.integers(0, 6, (16, V))])
    return pack(x, r, p, c, s, h)
def setup_inputs_ties(rng):
    x, r, p, c, s, h = parts(rng); sh = (N, 8, 16, V)
    x = 8 * rng.integers(0, 2, sh); pool = rng.integers(0, V, (N, 8, 1, 24)); pool[..., 0] = 0; pool[..., 1] = V - 1; pool[..., 2] = V; pool[..., 3] = W - 1
    few = np.take_along_axis(pool, rng.integers(0, 24, sh), 3); c[:, ::2] = few[:, ::2]
    m = np.arange(16)[:, None] == rng.integers(0, 16, (N, 8, 1, 1))
    r = np.where(m, rng.integers(100, 102, sh), rng.integers(101, 256, sh)); p = np.where(m, rng.integers(99, 101, sh), 0)
    h = deal(rng, [24, 32, 40, 48, 64])
    return pack(x, r, p, c, s, h)
def setup_inputs_border(rng):
    x, r, p, c, s, h = parts(rng); x = rng.integers(0, 256, x.shape); h = rng.integers(1, 33, h.shape); s[...] = np.arange(V)
    goal = np.zeros((N, 8, 3), np.int64); e, y, w = G - 1, V - 3, V - 2
    for q in range(N):
        for g in range(8):
            n, turn = ((0, 0), (0, int(rng.integers(1, 3))), (CAP - 1, 0), (CAP, 0), (CAP + 1, 0), (G, 0))[(g + q) % 6]
            o = [4 * rng.permutation(G // 4 - 1) + i for i in range(4)]
            v = o[turn][0]; j = o[0][1]; v1 = o[1][1]; u = o[1][2]; b = o[3][1]; z = o[3][2]
            for a in (v, e, j, y, v1, w, u, b): s[q, g, :, a] = z; c[q, g, :, a] = rng.integers(V, W, 16)
            for a in (v, v1, u): r[q, g, :, a] = rng.integers(140, 200, 16); p[q, g, :, a] = rng.integers(0, 41, 16)
            for a in (e, j): r[q, g, :, a] = rng.integers(200, 255, 16); p[q, g, :, a] = 0
            for a in (y, w): r[q, g, :, a] = 255; p[q, g, :, a] = 0
            r[q, g, :, z] = 255; r[q, g, :, V - 1] = 1
            i, k = rng.integers(0, 16, 2); d = int(rng.integers(1, 41))
            r[q, g, :, b] = r[q, g, :, u]; p[q, g, :, b] = p[q, g, :, u]; r[q, g, i, b] -= d; p[q, g, k, b] += d
            for a, f in ((v, e), (j, y), (v1, y), (w, y), (u, b)): x[q, g, :, a] = x[q, g, :, f]
            for a, f in ((v, e), (j, y), (v1, j), (w, y), (u, b)): c[q, g, int(rng.integers(0, 16)), a] = f
            a = rng.permutation(np.setdiff1d(np.arange(0, G, QB), np.array([v, j])))[:n]
            s[q, g][rng.integers(0, 16, len(a)), a] = V - 1
            goal[q, g] = (e, u, j)
    k = np.arange(G, V - 3)
    for q in range(N):
        for g in range(8):
            see = np.concatenate([V + goal[(q + 1) % N, g], V + G + goal[(q - 1) % N, g]])
            r[q, g, :, G:V - 3] = 255; p[q, g, :, G:V - 3] = 0
            s[q, g][rng.integers(0, 16, len(k)), k] = see[((k - G) // 4) % 6]
    return pack(x, r, p, c, s, h)
def setup_inputs_spread(rng):
    sh = (N, 8, 16, V); one = (N, 8, 1, V)
    def uneven(): return np.floor(np.exp2(8 * rng.random(one)) * rng.random(sh)).astype(np.int64)
    def lean():
        e = deal(rng, [1.0, 2.0, 4.0])[:, :, None, None]; v = np.minimum((W * rng.random(sh) ** e).astype(np.int64), W - 1)
        return np.where(deal(rng, [0, 0, 1])[:, :, None, None] == 1, W - 1 - v, v)
    x = uneven(); r = np.maximum(255 - uneven(), 1); p = np.where(rng.random(one) < 0.3, uneven(), 0)
    c = lean(); s = np.where(rng.random(one) < rng.random(sh), np.arange(V), lean())
    h = np.minimum(np.floor(np.exp2(12 * rng.random((N, 8)))).astype(np.int64), 4095)
    return pack(x, r, p, c, s, h)
def check_inputs(d):
    bad = []
    for k, lo, hi in (("x", 0, 255), ("reach", 1, 255), ("past", 0, 255), ("cand", 0, W - 1), ("succ", 0, W - 1), ("th", 0, 4095)):
        a = np.asarray(d[k]).astype(np.float64)
        if not (np.all(a >= lo) and np.all(a <= hi)): bad.append("range of " + k)
        elif not np.all(a == np.floor(a)): bad.append("whole numbers in " + k)
    return bad
def at(a, ix):
    return np.take_along_axis(a, ix[:, :, None, :], 3)
def reference(x, reach, past, cand, succ, th):
    X = x.astype(np.float32).astype(np.int32).reshape(N, 8, 16, V)
    R = reach.astype(np.float32).astype(np.int32).reshape(N, 8, 16, V); P = past.astype(np.float32).astype(np.int32).reshape(N, 8, 16, V)
    R = np.concatenate([R, np.roll(R[..., :G], -1, axis=0), np.roll(R[..., :G], 1, axis=0)], axis=3)
    P = np.concatenate([P, np.roll(P[..., :G], -1, axis=0), np.roll(P[..., :G], 1, axis=0)], axis=3)
    C = cand.astype(np.int64).reshape(N, 8, 16, V); S = succ.astype(np.int64).reshape(N, 8, 16, V); H = th.astype(np.int64).reshape(N, 8)
    F = np.zeros((N, 8, W), np.int64) + np.arange(W); M = np.zeros(N, np.int64); odd = (np.arange(16) % 2 == 1)[:, None]; NONE = 2 ** 20
    qi, gi = np.arange(N)[:, None, None], np.arange(8)[None, :, None]
    for t in range(RO):
        r_old, p_old, f_old = R[..., :G].copy(), P[..., :G].copy(), F[..., :G].copy()
        a = slice(t % QA, V, QA); v = np.arange(t % QA, V, QA); L = len(v)
        c = np.take_along_axis(F, C[..., a].reshape(N, 8, 16 * L), 2)
        xc, rc, pc = [at(w, i).reshape(N, 8, 16, 16, L) for w, i in ((X, np.minimum(c, V - 1)), (R, c), (P, c))]
        xv, rv, pv = [w[..., a][:, :, :, None, :] for w in (X, R, P)]
        c = c.reshape(N, 8, 16, L); ordered = np.any((rv <= pc) | (rc <= pv), axis=2)
        fit = ~ordered & (c < V) & (c % QA != t % QA)
        D = np.where(fit, np.add.reduce(np.abs(xc - xv), axis=2), NONE)
        k = np.argmin(D, axis=2)[:, :, None, :]
        b = np.take_along_axis(c, k, 2)[:, :, 0]; D = np.take_along_axis(D, k, 2)[:, :, 0].astype(np.int64); has = D < NONE; b = np.where(has, b, 0)
        C[..., a] = np.where(ordered & has[:, :, None, :], at(C, b), C[..., a])
        asks = has & (D < H[:, :, None] + (M & 31)[:, None, None]); key = np.where(asks, D * V + v, 2 ** 40)
        best = np.full((N, 8, V), 2 ** 40, np.int64); np.minimum.at(best, (qi, gi, b), key)
        win = asks & (np.take_along_axis(best, b, 2) == key); m = win[:, :, None, :]
        xb, rb, pb, sb = at(X, b), at(R, b), at(P, b), at(S, b)
        X[..., a] = np.where(m, (X[..., a] + xb) >> 1, X[..., a])
        R[..., a] = np.where(m, np.minimum(R[..., a], rb), R[..., a]); P[..., a] = np.where(m, np.maximum(P[..., a], pb), P[..., a])
        S[..., a] = np.where(m & odd, sb, S[..., a])
        i, j, l = np.nonzero(win); F[i, j, b[i, j, l]] = v[l]
        M = np.add.reduce(win.astype(np.int64).reshape(N, -1), axis=1)
        a = slice(t % QB, V, QB); L = len(range(t % QB, V, QB))
        c = np.take_along_axis(F, S[..., a].reshape(N, 8, 16 * L), 2)
        low = np.min(at(R, c).reshape(N, 8, 16, 16, L), axis=3); R[..., a] = np.minimum(R[..., a], low)
        ch = np.any(R[..., :G] != r_old, axis=2) | np.any(P[..., :G] != p_old, axis=2) | (F[..., :G] != f_old)
        go = ch & (np.add.accumulate(ch.astype(np.int64), axis=2) <= CAP)
        for turn, o in ((-1, V), (1, V + G)):
            w = np.roll(go, turn, axis=0); m = w[:, :, None, :]; f = np.roll(F[..., :G], turn, axis=0)
            R[..., o:o + G] = np.where(m, np.roll(R[..., :G], turn, axis=0), R[..., o:o + G])
            P[..., o:o + G] = np.where(m, np.roll(P[..., :G], turn, axis=0), P[..., o:o + G])
            F[..., o:o + G] = np.where(w & (f < G), f + o, F[..., o:o + G])
    return {"yx": X.reshape(N, 128, V).astype(np.float32).astype(BF), "yr": np.ascontiguousarray(R[..., :V]).reshape(N, 128, V).astype(np.float32).astype(BF), "yc": C.reshape(N, 128, V).astype(np.float32)}

@@ -1,0 +1,593 @@
+from concourse.bass import DstId, RemoteDMATransfer
+from concourse.mybir import AluOpType, AxisListType, ActivationFunctionType as AF
+
+V, G5, RO, CAP = 1024, 512, 4, 96
+DUM, GH, RAW, WID = 256, 1280, 2304, 3328
+PEN = 16384.0
+B10 = 10.0 * 2 ** 20
+TESTS = (("P", 0, "V"), ("P", 1, "V"), ("P", 2, "V"), ("R", 0, "V"), ("R", 1, "V"), ("P", 3, "V"), ("R", 2, "S"), ("R", 3, "S"))
+TESTS0 = tuple((k, i, "S" if (k, i) == ("R", 3) else "V") for k, i, _ in TESTS)
+SUCC = ((0, 1024), (1024, 2048), (2048, 3072), (3072, 4096))
+PAIRS = "SVSSVSSVSSVSSVSS"
+
+SCRATCH, PLACE = {}, {}
+SIZE = {"bfloat16": 2, "uint16": 2, "float32": 4, "int32": 4}
+
+
+def _b(names, cols, dtype, where="sbuf"):
+    for name in names.split():
+        if where == "sbuf" and cols <= 512:
+            pool = "pool_" + dtype
+            at = SCRATCH.get(pool, (where, [128, 0], dtype))[1][1]
+            step = 32 // SIZE[dtype]
+            SCRATCH[pool] = (where, [128, at + -(-cols // step) * step], dtype)
+            PLACE[name] = (pool, at, cols)
+        else:
+            SCRATCH[name] = (where, [128, cols], dtype)
+            PLACE[name] = (name, 0, cols)
+
+
+_b("xb rb pb", WID, "bfloat16")
+_b("fl vi nv", DUM + V, "float32"); _b("idf", 128, "float32")
+_b("ci si", V, "int32")
+_b("cb sb", V, "float32")
+for _t in range(RO):
+    _b("rr%d pr%d" % (_t, _t), 1024, "bfloat16")
+    _b("ct%d" % _t, 256, "uint16"); _b("ca%d" % _t, 256, "float32")
+    _b("xa%d rn%d pn%d" % (_t, _t, _t), 256, "bfloat16"); _b("z%d" % _t, 32, "uint16")
+    _b("lra%d lrb%d lpa%d lpb%d" % (_t, _t, _t, _t), 128, "bfloat16")
+    _b("lz%d" % _t, 64, "uint16")
+_b("xg ad tp tr sg sc gp", 4096, "bfloat16")
+_b("rwa rwb pwa pwb", 1024, "bfloat16")
+_b("rva rvb pva pvb", 512, "bfloat16")
+_b("wm", 2048, "bfloat16"); _b("em", 2048, "float32")
+_b("idm ngm bom ltm sb2m onm", 128, "bfloat16"); _b("b8", 128, "float32")
+_b("ia ib ic", 256, "int32"); _b("id_ ie ig ih ij ik in_", 128, "int32"); _b("iq", 1024, "int32")
+_b("pc", 8, "int32"); _b("cc", 48, "float32"); _b("g8", 8, "bfloat16"); _b("lh", 128, "bfloat16"); _b("lw", 16, "float32")
+_b("dg", 512, "bfloat16"); _b("thr sg1", 256, "float32"); _b("smx", 1024, "bfloat16")
+_b("kc cll clr", 256, "bfloat16"); _b("rq", 96, "bfloat16"); _b("one", 32, "float32")
+_b("o2 ofin oq omx", 16, "uint16"); _b("oke", 32, "uint16")
+_b("in12 tr12", 512, "float32")
+_b("key", 256, "int32"); _b("k8", 128, "int32"); _b("k4", 64, "int32"); _b("k2", 32, "int32"); _b("mk", 16, "int32")
+_b("eq prd", 256, "float32"); _b("s8", 128, "float32"); _b("s4", 64, "float32"); _b("s2", 32, "float32")
+_b("s1 has ask nli bc pen", 16, "float32"); _b("nl bcu", 16, "uint16"); _b("fsh fbt", 256, "int32")
+_b("bits fev fod fr junk we os", 256, "bfloat16"); _b("bm bs cd od sx sev", 256, "float32"); _b("kl", 32, "int32"); _b("ke", 512, "bfloat16")
+_b("mx", 16, "float32"); _b("nb3 d3 t3", 48, "float32"); _b("l3", 48, "uint16"); _b("v3", 192, "float32"); _b("so", 256, "uint16")
+_b("xs xh", 256, "int32"); _b("r2 nsm0 nsm1", 256, "bfloat16")
+_b("wn", 16, "bfloat16"); _b("mt", 2, "float32"); _b("mi", 2, "int32"); _b("thi", 8, "int32"); _b("thf", 8, "float32")
+_b("dr dp", 128, "bfloat16")
+_b("fls fvs e5 flt dfl c96 go ge gf zf", 32, "float32"); _b("fli", 32, "int32"); _b("chf ch scq", 32, "bfloat16")
+_b("zi fi ei jl", 64, "int32"); _b("fu eu", 64, "uint16")
+_b("p0 p1 p2 p3 p4 p5 p6 p7", 512, "float32", "psum")
+SEMAPHORES = ["qV", "qS", "qP", "qG", "inA", "inB"] + ["d%d" % i for i in range(24)] + ["ls%d" % i for i in range(12)] + \
+    ["%s%s%d" % (a, s, t) for a in ("ar", "ap", "az") for s in "AB" for t in range(RO - 1)]
+
+
+def rank_program(g, core, T, topo):
+    rank = T.rank_of(core)
+    if rank is None:
+        return
+    O = AluOpType
+    queues = {"V": g.vector, "S": g.scalar, "P": g.tensor, "G": g, "D": g.sync}
+    cnt = {"qV": 0, "qS": 0, "qP": 0, "qG": 0}
+    know = {q: {} for q in queues}
+    snap, hist, free = {}, {}, {"d": 0, "ls": 0}
+
+    def A(name, a=None, b=None, s=1, p0=0, p1=128):
+        buf, at, cols = PLACE[name]
+        t = T[buf]
+        a = 0 if a is None else a
+        b = cols if b is None else b
+        return {"n": name, "a": a, "b": b, "s": s, "ap": t[p0:p1, at + a:at + b:s] if s != 1 else t[p0:p1, at + a:at + b]}
+
+    def wait(q, sem, val):
+        if know[q].get(sem, 0) < val:
+            queues[q].wait_ge(T.sem[sem], val)
+            for k, v in snap.get((sem, val), {}).items():
+                if know[q].get(k, 0) < v: know[q][k] = v
+            know[q][sem] = val
+
+    def deps(q, reads, writes):
+        need = {}
+        for acc, w in [(r, False) for r in reads] + [(r, True) for r in writes]:
+            ps = SCRATCH[PLACE[acc["n"]][0]][0] == "psum"
+            for e in hist.get(acc["n"], ()):
+                if e[3] == q and ps and q == "P": continue
+                if (w or e[2] or (ps and e[3] != q)) and (ps or (acc["a"] < e[1] and e[0] < acc["b"])):
+                    if need.get(e[4], 0) < e[5]: need[e[4]] = e[5]
+        for s in sorted(need): wait(q, s, need[s])
+
+    def note(q, sem, val, reads, writes):
+        snap[(sem, val)] = dict(know[q])
+        for acc, w in [(r, False) for r in reads] + [(r, True) for r in writes]:
+            h = hist.setdefault(acc["n"], [])
+            if w and acc["s"] == 1:
+                h[:] = [e for e in h if not (acc["a"] <= e[0] and e[1] <= acc["b"])]
+            else:
+                h[:] = [e for e in h if not (e[4] == sem and e[2] == w and e[0] == acc["a"] and e[1] == acc["b"])]
+            h.append((acc["a"], acc["b"], w, q, sem, val))
+
+    def run(q, fn, writes, reads):
+        deps(q, reads, writes)
+        s = "q" + q
+        cnt[s] += 1
+        fn().then_inc(T.sem[s], 1)
+        note(q, s, cnt[s], reads, writes)
+
+    def dma(q, out, in_, reads, writes):
+        deps(q, reads, writes)
+        s = "d%d" % free["d"]; free["d"] += 1
+        queues[q].dma_start(out, in_).then_inc(T.sem[s], 16)
+        note(q, s, 16, reads, writes)
+
+    def ind(win, off): return {"ap": win["ap"].indirect(off["ap"]), "w": win, "o": off}
+    def rd(x): return [x["w"], x["o"]] if "w" in x else [x]
+    def cp(out, in_): run("V", lambda: g.vector.tensor_copy(out["ap"], in_["ap"]), [out], rd(in_))
+    def scat(win, off, in_): run("V", lambda: g.vector.tensor_copy(win["ap"].indirect(off["ap"]), in_["ap"]), [win], [off, in_])
+    def tt(out, a, b, op): run("V", lambda: g.vector.tensor_tensor(out["ap"], a["ap"], b["ap"], op), [out], rd(a) + [b])
+    def ts(out, a, s1, op0, s2=None, op1=None):
+        r = rd(a) + [s for s in (s1, s2) if isinstance(s, dict)]
+        v1 = s1["ap"] if isinstance(s1, dict) else s1
+        v2 = s2["ap"] if isinstance(s2, dict) else s2
+        if op1 is None: run("V", lambda: g.vector.tensor_scalar(out["ap"], a["ap"], v1, None, op0), [out], r)
+        else: run("V", lambda: g.vector.tensor_scalar(out["ap"], a["ap"], v1, v2, op0, op1), [out], r)
+    def scan(out, d0, d1, init, op0, op1): run("V", lambda: g.vector.tensor_tensor_scan(out["ap"], d0["ap"], d1["ap"], init, op0, op1), [out], [d0, d1])
+    def fill(out, v): run("V", lambda: g.vector.memset(out["ap"], v), [out], [])
+    def reduce(out, in_, op): run("V", lambda: g.vector.tensor_reduce(out["ap"], in_["ap"], AxisListType.X, op), [out], [in_])
+    def act(out, in_, func=AF.Copy, bias=0.0, scale=1.0, acc=None):
+        r = rd(in_) + ([scale] if isinstance(scale, dict) else [])
+        sc = scale["ap"] if isinstance(scale, dict) else scale
+        if acc is None: run("S", lambda: g.scalar.activation(out["ap"], in_["ap"], func, bias=bias, scale=sc), [out], r)
+        else: run("S", lambda: g.scalar.activation(out["ap"], in_["ap"], func, bias=bias, scale=sc, accum_out=acc["ap"]), [out, acc], r)
+    def mm(out, l, r, start, stop): run("P", lambda: g.tensor.matmul(out["ap"], l["ap"], r["ap"], start, stop), [out], [l, r])
+    def iota(out, pat, base=0, cm=0): run("G", lambda: g.iota(out["ap"], pat, base, cm), [out], [])
+    def iotf(out, pat, base=0, cm=0): run("G", lambda: g.iota(out["ap"], pat, base, cm, allow_small_or_imprecise_dtypes=True), [out], [])
+
+    nxt, prv = T.cores[(rank + 1) % 8], T.cores[(rank - 1) % 8]
+    far = [d for d in (nxt, prv) if topo.chip(d) != topo.chip(core)]
+    eng = {}
+    for d in (nxt, prv):
+        e = topo.engines(core, d)
+        if d not in far: e = [i for i in e if not far or i not in topo.engines(core, far[0])] or e
+        elif len(far) == 2: e = e[:len(e) // 2] if d == far[0] else e[len(e) // 2:]
+        eng[d] = e
+
+    def send(pairs, sems, n):
+        s = "ls%d" % free["ls"]; free["ls"] += 1
+        deps("G", [p[0] for p in pairs], [])
+        tr = []
+        for side, d in (("A", prv), ("B", nxt)):
+            rid, pid, _ = topo.addr(d)
+            for i, p in enumerate(pairs):
+                tr.append(RemoteDMATransfer(dst_ids=[DstId(rid=rid, pnc=pid)], dma_engine_mask=sum(1 << e for e in eng[d][i * n:i * n + n]),
+                                            remote_sem=T.sem[sems[i] % side], src=p[0]["ap"], dst=p[1 if side == "A" else 2]["ap"]))
+        g.remote_dma_fused(tr, local_sem=T.sem[s])
+        note("G", s, n * len(tr), [p[0] for p in pairs], [])
+
+    def arrive(sem, val, writes):
+        snap[(sem, val)] = {}
+        for w in writes: hist.setdefault(w["n"], []).append((w["a"], w["b"], True, "R", sem, val))
+
+    RWb = lambda n: A(n, RAW, RAW + V)
+    own = lambda n: A(n, DUM, GH)
+    gA, gB = (GH, GH + G5), (GH + G5, GH + 2 * G5)
+    dma("D", RWb("rb")["ap"], T.reach[:], [], [RWb("rb")])
+    dma("S", RWb("pb")["ap"], T.past[:], [], [RWb("pb")])
+    dma("D", A("ci")["ap"], T.cand[:], [], [A("ci")])
+    dma("S", own("xb")["ap"], T.x[:], [], [own("xb")])
+    dma("D", RWb("xb")["ap"], T.x[:], [], [RWb("xb")])
+    dma("D", own("rb")["ap"], T.reach[:], [], [own("rb")])
+    dma("D", own("pb")["ap"], T.past[:], [], [own("pb")])
+    dma("D", A("si")["ap"], T.succ[:], [], [A("si")])
+    dma("D", A("thi", 0, 1, p1=8)["ap"], T.th[:], [], [A("thi")])
+    c = lambda i: A("cc", i, i + 1)
+    ROW, P16, PF, ODD, SCL, RS, RG0, RG1, C1L, C1R, M12, M15, TH16, NG, LIM, EVR, W0, W1, W2, W3, W4 = range(21)
+    NRS, PM = 24, 28
+    rw, pp = A("pc", 1, 2), A("pc", 0, 1)
+    iota(pp, [[0, 1]], 0, 1)
+    iota(A("id_", 0, 16), [[32, 8], [-16, 2]], 16, 1)
+    iota(A("id_", 16, 32), [[1, 16]])
+    iota(A("ie"), [[1, 128]])
+    iota(A("ig", 0, 8), [[1, 8]])
+    iota(A("ia"), [[1, 16], [0, 16]])
+    iotf(A("xb", GH, RAW), [[0, RAW - GH]], int(PEN))
+    send([(A("rb", RAW, RAW + G5), A("rb", *gA), A("rb", *gB)), (A("pb", RAW, RAW + G5), A("pb", *gA), A("pb", *gB))], ["in%s", "in%s"], 4)
+    for n in ("rb", "pb"):
+        arrive("inA", 8, [A(n, *gA)]); arrive("inB", 8, [A(n, *gB)])
+    ts(rw, pp, 15, O.bitwise_and)
+    ts(A("pc", 2, 3), pp, 4, O.arith_shift_right)
+    ts(A("pc", 3, 4), pp, 4, O.arith_shift_right, 1, O.bitwise_and)
+    ts(A("pc", 4, 5), rw, 1, O.arith_shift_right)
+    ts(A("pc", 5, 6), rw, 1, O.bitwise_and)
+    cp(c(ROW), rw); cp(c(P16), A("pc", 2, 3)); cp(c(PF), pp); cp(c(RG1), A("pc", 3, 4)); cp(c(W0), A("pc", 4, 5)); cp(c(ODD), A("pc", 5, 6))
+    ts(c(RG0), c(RG1), -1.0, O.mult, 1.0, O.add)
+    ts(c(EVR), c(ODD), -1.0, O.mult, 1.0, O.add)
+    ts(c(NG), c(P16), -16.0, O.mult)
+    ts(A("o2"), A("id_", 0, 16), c(NG), O.add)
+    tt(c(W1), c(ODD), c(RG1), O.not_equal)
+    ts(c(W2), c(W0), 32.0, O.mult)
+    ts(c(W1), c(W1), 256.0, O.mult, c(W2), O.add)
+    ts(c(W2), c(RG1), 16.0, O.mult, c(W1), O.add)
+    ts(A("ofin"), A("id_", 16, 32), c(W2), O.add)
+    ts(A("idm"), A("ie"), c(PF), O.is_equal)
+    ts(A("ngm"), A("idm"), -1.0, O.mult)
+    ts(A("g8"), A("ig", 0, 8), c(P16), O.is_equal)
+    fill(A("wm"), 0.0)
+    for m in range(16): act(A("wm", 128 * m + m, 128 * m + 128, 16), A("g8"))
+    ts(A("kc"), A("ia"), 2.0 ** -23, O.mult)
+    fill(c(SCL), 1.0)
+    for b in range(4):
+        ts(A("pc", 7, 8), rw, b, O.arith_shift_right, 1, O.bitwise_and)
+        ts(c(W3), A("pc", 7, 8), 2.0 ** -(2 ** b) - 1.0, O.mult, 1.0, O.add)
+        tt(c(SCL), c(SCL), c(W3), O.mult)
+
+    def rows(i, parts):
+        for n, (op, lim, v) in enumerate(parts):
+            ts(c(i) if n == 0 else c(W3), c(ROW), float(lim), op, float(v), O.mult)
+            if n: tt(c(i), c(i), c(W3), O.add)
+    rows(RS, [(O.is_lt, 10, 2 ** 20)] + [(O.is_equal, r, v) for r, v in ((10, 2 ** 14), (11, 2 ** 8), (12, 1), (13, -2 ** 14), (14, -2 ** 8), (15, -1))])
+    rows(C1L, [(O.is_lt, 10, -1), (O.is_gt, 12, 1)])
+    rows(C1R, [(O.is_lt, 10, -2), (O.is_lt, 13, 1)])
+    ts(c(M12), c(ROW), 12.0, O.is_equal); ts(c(M15), c(ROW), 15.0, O.is_equal)
+    ts(c(W4), c(ROW), 10.0, O.is_lt, 2.0, O.mult)
+    ts(A("sb2m"), A("idm"), c(W4), O.mult)
+    cp(A("idf"), A("idm"))
+    fill(A("smx"), 0.0); fill(A("smx", 0, 1024, 16), 255.0)
+    fill(A("sg1"), 1.0); fill(A("sg1", 0, 256, 16), 0.0)
+    fill(A("nsm0"), 0.0)
+
+    def turn_a(t):
+        cp(A("in12", 0, 256), A("ci", t, V, 4))
+        act(A("in12", 256, 512), ind(A("in12", 0, 256), A("o2")))
+
+    def turn_b(t):
+        run("V", lambda: g.vector.transpose(A("tr12")["ap"], A("in12")["ap"]), [A("tr12")], [A("in12")])
+        act(A("ca%d" % t), ind(A("tr12"), A("ofin")))
+        cp(A("ct%d" % t), A("ca%d" % t))
+
+    def copies(t, f):
+        f(A("xa%d" % t), A("xb", RAW + t, RAW + V, 4))
+        for n in ("r", "p"):
+            for i in range(4): f(A("%sr%d" % (n, t), 256 * i, 256 * i + 256), A(n + "b", RAW + t, RAW + V, 4))
+
+    def squeeze(n, i, last):
+        for m in range(16):
+            mm(A("p4", 64 * i, 64 * i + 64), A("wm", 128 * m, 128 * m + 128), A(n, 1024 * i + m, 1024 * i + 1024, 16), False, last and m == 15)
+
+    def x_gather(t, i): act(A("xg", 1024 * i, 1024 * i + 1024), ind(A("xb", DUM, RAW), A("ct%d" % t, 64 * i, 64 * i + 64)))
+
+    def x_sub(t, i):
+        for h in (2 * i, 2 * i + 1):
+            p = "p%d" % (h % 4)
+            mm(A(p), A("idm"), A("xg", 512 * h, 512 * h + 512), True, False)
+            mm(A(p, 0, 256), A("ngm"), A("xa%d" % t), False, False)
+            mm(A(p, 256, 512), A("ngm"), A("xa%d" % t), False, True)
+
+    def distances(t):
+        mm(A("p4", 0, 256), A("idm"), A("kc"), True, False)
+        x_sub(t, 0)
+        for i in range(4):
+            if i < 3: x_sub(t, i + 1)
+            for h in (2 * i, 2 * i + 1): act(A("ad", 512 * h, 512 * h + 512), A("p%d" % (h % 4)), AF.Abs, scale=2.0 ** -19)
+            squeeze("ad", i, False)
+
+    def tests(t):
+        todo, tv, ns = [], 0.0, 0
+        for kind, i, who in TESTS if t else TESTS0:
+            if who == "V":
+                todo.append((tv, 0, kind, i)); tv += 1.6; todo.append((tv, 3, kind, i))
+            else:
+                at = ((0.0, 3.0, 4.0), (1.5, 5.5, 6.5), (4.0, 6.6, 7.6))[ns]; ns += 1
+                for step in (1, 2, 3): todo.append((at[step - 1], step, kind, i))
+        left = len(TESTS)
+        for _, step, kind, i in sorted(todo):
+            win = A("pb" if kind == "P" else "rb", DUM, RAW)
+            mine = ("rr%d" if kind == "P" else "pr%d") % t
+            n = {"P": "tp", "R": "tr"}[kind]
+            off = A("ct%d" % t, 64 * i, 64 * i + 64)
+            if step == 0:
+                tt(A(n, 1024 * i, 1024 * i + 1024), ind(win, off), A(mine), O.is_ge if kind == "P" else O.is_le)
+            elif step == 1:
+                act(A("gp", 1024 * i, 1024 * i + 1024), ind(win, off))
+            elif step == 2:
+                for h in (2 * i, 2 * i + 1):
+                    p = "p%d" % (h % 4)
+                    mm(A(p), A("idm"), A("gp", 512 * h, 512 * h + 512), True, False)
+                    mm(A(p), A("ngm"), A(mine, 0, 512), False, True)
+                    act(A(n, 512 * h, 512 * h + 512), A(p), AF.Relu, bias=1.0, scale=1.0 if kind == "P" else -1.0)
+            else:
+                left -= 1
+                squeeze(n, i, left == 0)
+
+    def tree(srcs, op):
+        for i in range(len(srcs) - 1):
+            w = 128 >> i
+            tt(A(srcs[i + 1]), A(srcs[i], 0, w), A(srcs[i], w, 2 * w), op)
+
+    def partner(t):
+        ts(A("key"), A("p4", 0, 256), 2.0 ** 23, O.mult, 2.0 ** 22, O.min)
+        tree(("key", "k8", "k4", "k2", "mk"), O.min)
+        tt(A("eq"), ind(A("mk"), A("oq")), A("key"), O.is_equal)
+        tt(A("prd"), A("eq"), A("ca%d" % t), O.mult)
+        ts(A("has"), A("mk"), 65536.0, O.is_lt)
+        tree(("prd", "s8", "s4", "s2", "s1"), O.add)
+        tt(A("nli"), A("s1"), A("has"), O.mult)
+        cp(A("nl"), A("nli"))
+        fw = A("fl", DUM, DUM + V)
+        ts(A("fsh"), ind(fw, A("nl")), c(SCL), O.mult, -0.5 + 2.0 ** -11, O.add)
+        ts(A("kl", 0, 16), A("mk"), 10, O.arith_shift_right, 63, O.bitwise_and)
+        ts(A("fbt"), A("fsh"), 1, O.bitwise_and)
+        ts(A("pen"), A("mk"), c(LIM), O.is_ge, 128.0, O.mult)
+        ts(A("kl", 16, 32), A("mk"), 4, O.arith_shift_right, 63, O.bitwise_and)
+        cp(A("bits"), A("fbt"))
+        tt(A("kl", 0, 16), A("kl", 0, 16), A("pen"), O.add)
+        tt(A("ke"), ind(A("kl"), A("oke")), A("dg"), O.mult)
+        for p, cl, r in (("p5", "cll", 10), ("p6", "clr", 13)):
+            mm(A(p, 0, 256), A("idm"), A(cl), True, False)
+            mm(A(p, 0, 256), A("sb2m"), A("bits"), False, False)
+            mm(A(p, 0, 256), A("wm", 128 * r, 128 * r + 128), A("ke", 0, 256), False, False)
+            mm(A(p, 0, 256), A("wm", 128 * r + 128, 128 * r + 256), A("ke", 256, 512), False, True)
+        act(A("fr"), A("p6", 0, 256), scale=c(RS))
+        act(A("fev"), A("p5", 0, 256), scale=c(RG0))
+        ts(A("fod"), A("p5", 0, 256), c(RG1), O.mult)
+        seen = {"V": 0, "S": 0}
+        for a in range(16):
+            gr, h, who = a // 2, a % 2, PAIRS[a]
+            p = {"V": ("p0", "p2", "p5"), "S": ("p1", "p3", "p6")}[who][seen[who] % 3]
+            seen[who] += 1
+            lo = 32 * (gr // 2)
+            mm(A(p, 0, 256), A("fod" if gr % 2 else "fev", 128 * h, 128 * h + 128, p0=lo, p1=lo + 32), A("fr", p0=lo, p1=lo + 32), True, True)
+            if who == "V": reduce(A("mx", a, a + 1), A(p, 0, 256), O.max)
+            else: act(A("junk"), A(p, 0, 256), AF.Relu, bias=-B10, acc=A("mx", a, a + 1))
+        tt(A("bm"), ind(fw, A("nl")), A("dg", 0, 256), O.mult)
+        scan(A("bs"), A("sg1"), A("bm"), 0.0, O.mult, O.add)
+        v3 = A("v3", 48 * t, 48 * t + 48)
+        cp(A("nb3", 0, 16), A("nli"))
+        ts(A("nb3", 16, 32), A("bs", 15, 256, 16), float(DUM), O.add)
+        cp(A("nb3", 32, 48), A("bs", 15, 256, 16))
+        tt(A("d3"), A("nb3"), v3, O.subtract)
+        tt(A("bc"), A("d3", 32, 48), A("has"), O.mult)
+        tt(A("bc"), A("bc"), A("v3", 48 * t + 32, 48 * t + 48), O.add)
+        ts(A("ask"), A("mk"), c(LIM), O.is_lt)
+        for i in range(3): tt(A("d3", 16 * i, 16 * i + 16), A("d3", 16 * i, 16 * i + 16), A("ask"), O.mult)
+        cp(A("bcu"), A("bc"))
+        tt(A("we"), ind(A("mx"), A("omx")), A("thr"), O.is_le)
+        for h in range(2): mm(A("p7", 0, 48), A("we", 128 * h, 128 * h + 128), A("rq", 48 * h, 48 * h + 48), h == 0, h == 1)
+        tt(A("t3"), A("p7", 0, 48), A("d3"), O.mult)
+        tt(A("t3"), A("t3"), v3, O.add)
+        cp(A("l3"), A("t3"))
+
+    nl2, sc, sl = A("l3", 0, 16), A("l3", 16, 32), A("l3", 32, 48)
+
+    def selfmark(n, t, new, p, sign, op):
+        w = A(n, DUM + t, GH, 4)
+        mm(A(p, 0, 256), A("idm"), new, True, False)
+        mm(A(p, 0, 256), A(sign), A("nsm%d" % (t % 2)), False, True)
+        tt(w, w, A(p, 0, 256), op)
+
+    def merge(t):
+        tt(A("r2"), ind(A("rb", DUM, WID), nl2), A("rr%d" % t, 0, 256), O.min)
+        ts(A("sx"), ind(A("sb"), sl), c(ODD), O.mult)
+        scat(A("rb", 0, GH), sc, A("r2"))
+        tt(A("sb", t, V, 4), A("sx"), A("sev"), O.add)
+        cp(A("so"), A("sb", t, V, 4))
+        selfmark("rb", t, A("r2"), "p1", "idm", O.min)
+
+    def succ_gather(chunks):
+        for a, b in chunks: act(A("sg", a, b), ind(A("rb", DUM, RAW), A("so", a // 16, b // 16)))
+
+    def succ_min(t):
+        for a, b in SUCC: scan(A("sc", a, b), A("smx", 0, b - a), A("sg", a, b), 255.0, O.max, O.min)
+        tt(A("rn%d" % t), A("sc", 15, 4096, 16), A("r2"), O.min)
+
+    def pmerge(t): tt(A("pn%d" % t), ind(A("pb", DUM, WID), nl2), A("pr%d" % t, 0, 256), O.max)
+
+    def xmerge(t):
+        tt(A("xs"), ind(A("xb", DUM, WID), nl2), A("xa%d" % t), O.add)
+        ts(A("xh"), A("xs"), 1, O.arith_shift_right)
+        cp(A("xb", RAW + t, RAW + V, 4), A("xh"))
+
+    def c_flags():
+        for k in range(16): mm(A("p5", 0, 256), A("wm", 128 * k, 128 * k + 128), A("tp", 256 * k, 256 * k + 256), k == 0, False)
+        for k in range(16): mm(A("p5", 0, 256), A("wm", 128 * k, 128 * k + 128), A("tr", 256 * k, 256 * k + 256), False, k == 15)
+        act(A("os"), A("p5", 0, 256), AF.Sign)
+
+    def c_update(t):
+        tt(A("cd"), ind(A("cb"), A("bcu")), A("ci", t, V, 4), O.subtract)
+        tt(A("od"), A("os"), A("cd"), O.mult)
+        tt(A("cb", t, V, 4), A("cb", t, V, 4), A("od"), O.add)
+
+    def marks(u):
+        ns = A("nsm%d" % (u % 2))
+        mm(A("p2", 0, 256), A("idf"), A("fl", DUM + u, DUM + V, 4), True, False)
+        mm(A("p2", 0, 256), A("idf"), A("nv", DUM + u, DUM + V, 4), False, True)
+        act(ns, A("p2", 0, 256), AF.Abs, scale=PEN)
+        act(A("p3", 0, 256), ns, AF.Relu, bias=PEN, scale=-1.0)
+
+    def windows(t):
+        xr, u = A("xb", RAW + t, RAW + V, 4), t + 1
+        scat(A("xb", 0, GH), sc, xr)
+        selfmark("xb", t, xr, "p0", "idm", O.min)
+        pwin(t)
+        f_changes(t)
+        tt(A("xb", DUM + u, GH, 4), A("xb", DUM + u, GH, 4), A("p3", 0, 256), O.max)
+
+    def f_list(t):
+        for m in range(16): mm(A("p6", 0, 32), A("em", 128 * m, 128 * m + 128), A("fl", DUM + m, DUM + G5, 16), m == 0, m == 15)
+
+    def f_changes(t):
+        cp(A("fls"), A("p6", 0, 32)); cp(A("fli"), A("fls"))
+        tt(A("dp"), A("pn%d" % t, 0, 128), A("pr%d" % t, 0, 128), O.not_equal)
+        ts(A("flt"), A("fls"), float(G5), O.is_lt)
+        ts(A("fli"), A("fli"), 3, O.bitwise_and)
+        tt(A("dfl"), A("fls"), A("fvs"), O.subtract)
+        ts(A("chf"), A("fli"), float(t), O.is_equal, c(NRS + t), O.mult)
+        tt(A("dfl"), A("dfl"), A("flt"), O.mult)
+        mm(A("p7", 128, 160), A("idm"), A("chf"), True, False)
+        changed("dp", t, False)
+
+    def changed(n, t, last):
+        for a in range(4):
+            m = 4 * a + t
+            mm(A("p7", 128, 160), A("wm", 128 * m, 128 * m + 128), A(n, a, 128, 4), False, last and a == 3)
+
+    def publish(t):
+        tt(A("dr"), A("rn%d" % t, 0, 128), A("rr%d" % t, 0, 128), O.not_equal)
+        changed("dr", t, True)
+        ts(A("ch"), A("p7", 128, 160), 0.0, O.is_gt)
+        scan(A("scq"), A("one"), A("ch"), 0.0, O.mult, O.add)
+        ts(A("c96"), A("ch"), float(CAP + 1), O.mult, -1.0, O.add)
+        mm(A("p7", 192, 224), A("ltm"), A("ch"), True, False)
+        mm(A("p7", 192, 224), A("bom"), A("scq"), False, True)
+        tt(A("go"), A("p7", 192, 224), A("c96"), O.is_le)
+        ts(A("ge"), A("go"), c(PM + t), O.mult)
+        tt(A("gf"), A("go"), A("dfl"), O.mult)
+        tt(A("e5"), A("e5"), A("ge"), O.max)
+        tt(A("fvs"), A("fvs"), A("gf"), O.add)
+        tt(A("zf"), A("e5"), A("fvs"), O.add)
+        cp(A("z%d" % t), A("zf"))
+        send([(A("z%d" % t), A("lz%d" % t, 0, 32), A("lz%d" % t, 32, 64))], ["az%%s%d" % t], 2)
+
+    def pwin(t):
+        scat(A("pb", 0, GH), sc, A("pn%d" % t))
+        selfmark("pb", t, A("pn%d" % t), "p2", "ngm", O.max)
+
+    def rwin(t):
+        scat(A("rb", 0, GH), sc, A("rn%d" % t))
+        selfmark("rb", t, A("rn%d" % t), "p1", "idm", O.min)
+        ts(A("sev"), A("si", t + 1, V, 4), c(EVR), O.mult)
+        act(A("rb", RAW + t, RAW + V, 4), A("rn%d" % t))
+
+    def count(t):
+        tt(A("wn"), A("p7", 0, 16), A("ask"), O.mult)
+        mm(A("p7", 256, 272), A("onm"), A("wn"), True, True)
+        reduce(A("mt", 0, 1), A("p7", 256, 272), O.add)
+        cp(A("mi", 0, 1), A("mt", 0, 1))
+        ts(A("mi", 1, 2), A("mi", 0, 1), 31, O.bitwise_and)
+        ts(c(LIM), A("mi", 1, 2), 16.0, O.mult, c(TH16), O.add)
+
+    def block(kind, t):
+        n = "%sn%d" % (kind, t)
+        send([(A(n, 0, 128), A("l%sa%d" % (kind, t)), A("l%sb%d" % (kind, t)))], ["a%s%%s%d" % (kind, t)], 2)
+        for s, S in (("a", "A"), ("b", "B")): arrive("a%s%s%d" % (kind, S, t), 2, [A("l%s%s%d" % (kind, s, t))])
+
+    def ghosts(t):
+        arrive("azA%d" % t, 2, [A("lz%d" % t, 0, 32)]); arrive("azB%d" % t, 2, [A("lz%d" % t, 32, 64)])
+        for s in "ab":
+            act(A("rw" + s, G5 + t, 2 * G5, 4), A("lr%s%d" % (s, t)))
+            act(A("pw" + s, G5 + t, 2 * G5, 4), A("lp%s%d" % (s, t)))
+        cp(A("zi"), A("lz%d" % t))
+        ts(A("ei"), A("zi"), 512, O.bitwise_and)
+        ts(A("fi"), A("zi"), 511, O.bitwise_and)
+        tt(A("ei"), A("ei"), A("jl"), O.add)
+        cp(A("fu"), A("fi"))
+        cp(A("eu"), A("ei"))
+        for i, s in enumerate("ab"):
+            act(A("pv" + s), ind(A("pw" + s), A("eu", 32 * i, 32 * i + 32)))
+            cp(A("rv" + s), ind(A("rw" + s), A("eu", 32 * i, 32 * i + 32)))
+        for i, (s, w) in enumerate((("a", gA), ("b", gB))):
+            act(A("pb", *w), ind(A("pv" + s), A("fu", 32 * i, 32 * i + 32)))
+            cp(A("rb", *w), ind(A("rv" + s), A("fu", 32 * i, 32 * i + 32)))
+
+    turn_a(0)
+    fill(A("xb", DUM, GH, 4), PEN)
+    turn_b(0)
+    turn_a(1); turn_b(1)
+    copies(0, cp)
+    iota(A("ik"), [[1, 8], [0, 16]])
+    ts(A("b8"), A("ik"), c(PF), O.is_equal)
+    cp(A("thf", 0, 1, p1=8), A("thi", 0, 1, p1=8))
+    mm(A("p7", 0, 1), A("b8", p1=8), A("thf", 0, 1, p1=8), True, True)
+    ts(c(TH16), A("p7", 0, 1), 16.0, O.mult)
+    cp(c(LIM), c(TH16))
+    for i in range(4): x_gather(0, i)
+    distances(0)
+    iota(A("ib"), [[0, 16], [1, 16]])
+    iota(A("ic"), [[1, 256]])
+    iota(A("ih", 0, 16), [[1, 2], [2, 8]]); iota(A("ih", 16, 48), [[1, 32]])
+    iota(A("ij", 0, 16), [[0, 16]], 0, 1); iota(A("ij", 16, 32), [[16, 16]], 0, 1)
+    iotf(A("vi"), [[1, DUM + V]], -DUM); iotf(A("fl"), [[1, DUM + V]], -DUM); iotf(A("nv"), [[-1, DUM + V]], DUM)
+    iota(A("in_", 0, 96), [[-8, 2], [0, 3], [1, 16]])
+    iota(A("id_", 32, 96), [[0, 2], [16, 32]], 0, 1)
+    iotf(A("em"), [[0, 2048]])
+    ts(A("dg", 0, 256), A("ib"), c(ROW), O.is_equal); ts(A("dg", 256, 512), A("ib"), c(ROW), O.is_equal)
+    cp(A("oke"), A("ih", 16, 48)); cp(A("omx"), A("ih", 0, 16))
+    ts(A("oq"), A("ij", 0, 16), c(NG), O.add)
+    ts(A("cll"), A("ic"), c(M12), O.mult, c(C1L), O.add)
+    ts(A("clr"), A("ic"), c(M15), O.mult, c(C1R), O.add)
+    for a in range(16):
+        o = 128 * (a % 2) + 16 * (a // 2)
+        if a == 0: ts(A("thr"), A("dg", 0, 256), 1e9 + 0.5, O.mult, -1e9, O.add)
+        if PAIRS[a] == "V": ts(A("thr", o, o + 16), A("dg", 0, 16), 1e9 + B10, O.mult, -1e9, O.add)
+    ts(A("rq"), A("in_", 0, 96), c(P16), O.is_equal)
+    ts(A("lw"), A("ij", 16, 32), c(NG), O.add)
+    for t in range(RO):
+        o = 48 * t
+        ts(A("v3", o, o + 16), A("lw"), 4.0, O.mult, float(2048 + t), O.add)
+        cp(A("v3", o + 16, o + 32), A("lw"))
+        ts(A("v3", o + 32, o + 48), A("lw"), 4.0, O.mult, float(t), O.add)
+    cp(A("sb"), A("si"))
+    ts(A("sev"), A("si", 0, V, 4), c(EVR), O.mult)
+    for n in ("r", "p"):
+        for s, w in (("a", gA), ("b", gB)):
+            for o in (0, G5):
+                dma("D", A(n + "w" + s, o, o + G5)["ap"], A(n + "b", *w)["ap"], [A(n + "b", *w)], [A(n + "w" + s, o, o + G5)])
+
+    def border():
+        for m in range(16): act(A("em", 128 * m + m, 128 * m + 128, 16), A("idm", m, 128, 16))
+        ts(A("bom"), A("ik"), c(P16), O.is_equal)
+        ts(A("lh"), A("ie"), c(PF), O.is_lt, -1.0, O.mult)
+        tt(A("ltm"), A("lh"), A("bom"), O.mult)
+        ts(A("jl"), A("id_", 32, 96), c(NG), O.add)
+        cp(A("fvs"), A("jl", 0, 32)); fill(A("e5"), 0.0)
+        fill(A("one"), 1.0); fill(A("onm"), 1.0)
+        ts(A("pc", 7, 8), rw, 3, O.bitwise_and)
+        cp(c(W3), A("pc", 7, 8))
+        for t in range(RO - 1):
+            ts(c(NRS + t), c(W3), float(t), O.not_equal)
+            ts(c(PM + t), c(W3), float(t), O.is_le, 512.0, O.mult)
+
+    for t in range(RO):
+        last = t == RO - 1
+        tests(t)
+        c_flags()
+        if not last: copies(t + 1, act)
+        if t == 0: border()
+        partner(t)
+        merge(t)
+        if last:
+            succ_gather(SUCC)
+        else:
+            scat(A("fl", 0, DUM + V), sc, A("vi", DUM + t, DUM + V, 4))
+            if t + 2 < RO: turn_a(t + 2)
+            succ_gather(SUCC[:2])
+            marks(t + 1)
+            succ_gather(SUCC[2:])
+            pmerge(t)
+            block("p", t)
+            f_list(t)
+        xmerge(t)
+        if t == 0: cp(A("cb"), A("ci"))
+        if last:
+            dma("D", T.yx[:], RWb("xb")["ap"], [RWb("xb")], [])
+            c_update(t)
+            dma("D", T.yc[:], A("cb")["ap"], [A("cb")], [])
+            succ_min(t)
+            cp(A("rb", RAW + t, RAW + V, 4), A("rn%d" % t))
+            dma("D", T.yr[:], RWb("rb")["ap"], [RWb("rb")], [])
+            continue
+        windows(t)
+        if t + 2 < RO: turn_b(t + 2)
+        for i in range(4): x_gather(t + 1, i)
+        succ_min(t)
+        block("r", t)
+        publish(t)
+        rwin(t)
+        distances(t + 1)
+        c_update(t)
+        ghosts(t)
+        count(t)
+    for i in range(free["ls"]):
+        for (s, v) in [k for k in snap if k[0] == "ls%d" % i]: wait("G", s, v)
+    for s in sorted(cnt): wait("G", s, cnt[s])
+    for i in range(free["d"]): wait("D", "d%d" % i, 16)

@@ -5,10 +5,10 @@ V, G5, RO, CAP = 1024, 512, 4, 96
 DUM, GH, RAW, WID = 256, 1280, 2304, 3328
 PEN = 16384.0
 B10 = 10.0 * 2 ** 20
-TESTS = (("P", 0, "V"), ("P", 1, "V"), ("P", 2, "V"), ("R", 0, "V"), ("R", 1, "V"), ("P", 3, "V"), ("R", 2, "S"), ("R", 3, "S"))
-TESTS0 = tuple((k, i, "S" if (k, i) == ("R", 3) else "V") for k, i, _ in TESTS)
+TESTS = (("P", 0, 2, "V"), ("P", 2, 2, "V"), ("P", 4, 2, "V"), ("P", 6, 2, "V"), ("R", 0, 2, "V"), ("R", 2, 1, "V"), ("R", 3, 1, "S"), ("R", 4, 2, "S"), ("R", 6, 2, "S"))
+TESTS0 = tuple((k, i, n, "S" if (k, i) == ("R", 6) else "V") for k, i, n, _ in TESTS)
 SUCC = ((0, 1024), (1024, 2048), (2048, 3072), (3072, 4096))
-PAIRS = "SVSSVSSVSSVSSVSS"
+PAIRS = "SVSVSVSVSVSVSVSV"
 
 SCRATCH, PLACE = {}, {}
 SIZE = {"bfloat16": 2, "uint16": 2, "float32": 4, "int32": 4}
@@ -42,7 +42,8 @@ _b("rwa rwb pwa pwb", 1024, "bfloat16")
 _b("rva rvb pva pvb", 512, "bfloat16")
 _b("wm", 2048, "bfloat16"); _b("em", 2048, "float32")
 _b("idm ngm bom ltm sb2m onm", 128, "bfloat16"); _b("b8", 128, "float32")
-_b("ia ib ic", 256, "int32"); _b("id_ ie ig ih ij ik in_", 128, "int32"); _b("iq", 1024, "int32")
+_b("sc10 sc13 sw " + " ".join("se%d" % r for r in range(10, 16)), 1, "float32"); _b("ic", 256, "float32")
+_b("ia ib", 256, "int32"); _b("id_ ie ig ih ij ik in_", 128, "int32"); _b("iq", 1024, "int32")
 _b("pc", 8, "int32"); _b("cc", 48, "float32"); _b("g8", 8, "bfloat16"); _b("lh", 128, "bfloat16"); _b("lw", 16, "float32")
 _b("dg", 512, "bfloat16"); _b("thr sg1", 256, "float32"); _b("smx", 1024, "bfloat16")
 _b("kc cll clr", 256, "bfloat16"); _b("rq", 96, "bfloat16"); _b("one", 32, "float32")
@@ -56,7 +57,7 @@ _b("mx", 16, "float32"); _b("nb3 d3 t3", 48, "float32"); _b("l3", 48, "uint16");
 _b("xs xh", 256, "int32"); _b("r2 nsm0 nsm1", 256, "bfloat16")
 _b("wn", 16, "bfloat16"); _b("mt", 2, "float32"); _b("mi", 2, "int32"); _b("thi", 8, "int32"); _b("thf", 8, "float32")
 _b("dr dp", 128, "bfloat16")
-_b("fls fvs e5 flt dfl c96 go ge gf zf", 32, "float32"); _b("fli", 32, "int32"); _b("chf ch scq", 32, "bfloat16")
+_b("fvs e5 flt dfl c96 go ge gf zf", 32, "float32"); _b("fli", 32, "int32"); _b("chf ch scq", 32, "bfloat16")
 _b("zi fi ei jl", 64, "int32"); _b("fu eu", 64, "uint16")
 _b("p0 p1 p2 p3 p4 p5 p6 p7", 512, "float32", "psum")
 SEMAPHORES = ["qV", "qS", "qP", "qG", "inA", "inB"] + ["d%d" % i for i in range(24)] + ["ls%d" % i for i in range(12)] + \
@@ -135,9 +136,10 @@ def rank_program(g, core, T, topo):
     def fill(out, v): run("V", lambda: g.vector.memset(out["ap"], v), [out], [])
     def reduce(out, in_, op): run("V", lambda: g.vector.tensor_reduce(out["ap"], in_["ap"], AxisListType.X, op), [out], [in_])
     def act(out, in_, func=AF.Copy, bias=0.0, scale=1.0, acc=None):
-        r = rd(in_) + ([scale] if isinstance(scale, dict) else [])
+        r = rd(in_) + [k for k in (bias, scale) if isinstance(k, dict)]
         sc = scale["ap"] if isinstance(scale, dict) else scale
-        if acc is None: run("S", lambda: g.scalar.activation(out["ap"], in_["ap"], func, bias=bias, scale=sc), [out], r)
+        bi = bias["ap"] if isinstance(bias, dict) else bias
+        if acc is None: run("S", lambda: g.scalar.activation(out["ap"], in_["ap"], func, bias=bi, scale=sc), [out], r)
         else: run("S", lambda: g.scalar.activation(out["ap"], in_["ap"], func, bias=bias, scale=sc, accum_out=acc["ap"]), [out, acc], r)
     def mm(out, l, r, start, stop): run("P", lambda: g.tensor.matmul(out["ap"], l["ap"], r["ap"], start, stop), [out], [l, r])
     def iota(out, pat, base=0, cm=0): run("G", lambda: g.iota(out["ap"], pat, base, cm), [out], [])
@@ -209,50 +211,63 @@ def rank_program(g, core, T, topo):
     ts(c(W1), c(W1), 256.0, O.mult, c(W2), O.add)
     ts(c(W2), c(RG1), 16.0, O.mult, c(W1), O.add)
     ts(A("ofin"), A("id_", 16, 32), c(W2), O.add)
-    ts(A("idm"), A("ie"), c(PF), O.is_equal)
-    ts(A("ngm"), A("idm"), -1.0, O.mult)
-    ts(A("g8"), A("ig", 0, 8), c(P16), O.is_equal)
-    fill(A("wm"), 0.0)
-    for m in range(16): act(A("wm", 128 * m + m, 128 * m + 128, 16), A("g8"))
-    ts(A("kc"), A("ia"), 2.0 ** -23, O.mult)
-    fill(c(SCL), 1.0)
-    for b in range(4):
-        ts(A("pc", 7, 8), rw, b, O.arith_shift_right, 1, O.bitwise_and)
-        ts(c(W3), A("pc", 7, 8), 2.0 ** -(2 ** b) - 1.0, O.mult, 1.0, O.add)
-        tt(c(SCL), c(SCL), c(W3), O.mult)
+    def tables():
+        ts(A("g8"), A("ig", 0, 8), c(P16), O.is_equal)
+        fill(A("wm"), 0.0)
+        for m in range(16): act(A("wm", 128 * m + m, 128 * m + 128, 16), A("g8"))
+        ts(A("idm"), A("ie"), c(PF), O.is_equal)
+        ts(A("ngm"), A("idm"), -1.0, O.mult)
+        ts(A("kc"), A("ia"), 2.0 ** -23, O.mult)
+        fill(A("smx"), 0.0); fill(A("smx", 0, 1024, 16), 255.0)
+        fill(A("sg1"), 1.0); fill(A("sg1", 0, 256, 16), 0.0)
+        fill(A("nsm0"), 0.0)
 
-    def rows(i, parts):
-        for n, (op, lim, v) in enumerate(parts):
-            ts(c(i) if n == 0 else c(W3), c(ROW), float(lim), op, float(v), O.mult)
-            if n: tt(c(i), c(i), c(W3), O.add)
-    rows(RS, [(O.is_lt, 10, 2 ** 20)] + [(O.is_equal, r, v) for r, v in ((10, 2 ** 14), (11, 2 ** 8), (12, 1), (13, -2 ** 14), (14, -2 ** 8), (15, -1))])
-    rows(C1L, [(O.is_lt, 10, -1), (O.is_gt, 12, 1)])
-    rows(C1R, [(O.is_lt, 10, -2), (O.is_lt, 13, 1)])
-    ts(c(M12), c(ROW), 12.0, O.is_equal); ts(c(M15), c(ROW), 15.0, O.is_equal)
-    ts(c(W4), c(ROW), 10.0, O.is_lt, 2.0, O.mult)
-    ts(A("sb2m"), A("idm"), c(W4), O.mult)
-    cp(A("idf"), A("idm"))
-    fill(A("smx"), 0.0); fill(A("smx", 0, 1024, 16), 255.0)
-    fill(A("sg1"), 1.0); fill(A("sg1", 0, 256, 16), 0.0)
-    fill(A("nsm0"), 0.0)
+    def row_tables():
+        fill(c(SCL), 1.0)
+        for b in range(4):
+            ts(A("pc", 7, 8), rw, b, O.arith_shift_right, 1, O.bitwise_and)
+            ts(c(W3), A("pc", 7, 8), 2.0 ** -(2 ** b) - 1.0, O.mult, 1.0, O.add)
+            tt(c(SCL), c(SCL), c(W3), O.mult)
+        eq, lt = {}, {}
+        for lim in (10, 13):
+            lt[lim] = A("sc%d" % lim)
+            act(A("sw"), c(ROW), AF.Sign, bias=lim - 0.5, scale=-1.0)
+            act(lt[lim], A("sw"), AF.Relu)
+        for r in (10, 11, 12, 13, 14, 15):
+            eq[r] = A("se%d" % r)
+            act(A("sw"), c(ROW), AF.Abs, bias=-float(r))
+            act(eq[r], A("sw"), AF.Relu, bias=1.0, scale=-1.0)
+
+        def total(i, parts):
+            for n, (m, v) in enumerate(parts):
+                act(c(i), m, AF.Identity, bias=c(i) if n else 0.0, scale=float(v))
+        total(RS, [(lt[10], 2 ** 20), (eq[10], 2 ** 14), (eq[11], 2 ** 8), (eq[12], 1), (eq[13], -2 ** 14), (eq[14], -2 ** 8), (eq[15], -1)])
+        total(C1L, [(lt[10], -1), (eq[13], 1), (eq[14], 1), (eq[15], 1)])
+        total(C1R, [(lt[10], -2), (lt[13], 1)])
+        act(c(W4), lt[10], scale=2.0)
+        act(A("cll"), A("ic"), AF.Identity, bias=c(C1L), scale=eq[12])
+        act(A("clr"), A("ic"), AF.Identity, bias=c(C1R), scale=eq[15])
+        act(A("sb2m"), A("idm"), scale=c(W4))
+        act(A("idf"), A("idm"))
 
     def turn_a(t):
         cp(A("in12", 0, 256), A("ci", t, V, 4))
         act(A("in12", 256, 512), ind(A("in12", 0, 256), A("o2")))
 
-    def turn_b(t):
-        run("V", lambda: g.vector.transpose(A("tr12")["ap"], A("in12")["ap"]), [A("tr12")], [A("in12")])
-        act(A("ca%d" % t), ind(A("tr12"), A("ofin")))
-        cp(A("ct%d" % t), A("ca%d" % t))
+    def turn_v(t): run("V", lambda: g.vector.transpose(A("tr12")["ap"], A("in12")["ap"]), [A("tr12")], [A("in12")])
+
+    def turn_s(t): act(A("ca%d" % t), ind(A("tr12"), A("ofin")))
+
+    def list_b(t): cp(A("ct%d" % t), A("ca%d" % t))
 
     def copies(t, f):
         f(A("xa%d" % t), A("xb", RAW + t, RAW + V, 4))
         for n in ("r", "p"):
             for i in range(4): f(A("%sr%d" % (n, t), 256 * i, 256 * i + 256), A(n + "b", RAW + t, RAW + V, 4))
 
-    def squeeze(n, i, last):
+    def squeeze(n, i, w, last):
         for m in range(16):
-            mm(A("p4", 64 * i, 64 * i + 64), A("wm", 128 * m, 128 * m + 128), A(n, 1024 * i + m, 1024 * i + 1024, 16), False, last and m == 15)
+            mm(A("p4", 32 * i, 32 * (i + w)), A("wm", 128 * m, 128 * m + 128), A(n, 512 * i + m, 512 * (i + w), 16), False, last and m == 15)
 
     def x_gather(t, i): act(A("xg", 1024 * i, 1024 * i + 1024), ind(A("xb", DUM, RAW), A("ct%d" % t, 64 * i, 64 * i + 64)))
 
@@ -269,35 +284,38 @@ def rank_program(g, core, T, topo):
         for i in range(4):
             if i < 3: x_sub(t, i + 1)
             for h in (2 * i, 2 * i + 1): act(A("ad", 512 * h, 512 * h + 512), A("p%d" % (h % 4)), AF.Abs, scale=2.0 ** -19)
-            squeeze("ad", i, False)
+            squeeze("ad", 2 * i, 2, False)
 
     def tests(t):
-        todo, tv, ns = [], 0.0, 0
-        for kind, i, who in TESTS if t else TESTS0:
+        todo, tv, tg = [], 0.0, 0.0
+        plan = TESTS if t else TESTS0
+        for kind, i, n, who in plan:
             if who == "V":
-                todo.append((tv, 0, kind, i)); tv += 1.6; todo.append((tv, 3, kind, i))
+                todo.append((tv, 0, kind, i, n)); tv += 0.8 * n; todo.append((tv, 3, kind, i, n))
             else:
-                at = ((0.0, 3.0, 4.0), (1.5, 5.5, 6.5), (4.0, 6.6, 7.6))[ns]; ns += 1
-                for step in (1, 2, 3): todo.append((at[step - 1], step, kind, i))
-        left = len(TESTS)
-        for _, step, kind, i in sorted(todo):
+                todo.append((tg, 1, kind, i, n)); tg += 0.8 * n
+        for kind, i, n, who in plan:
+            if who == "S":
+                todo.append((tg, 2, kind, i, n)); tg += 0.65 * n; todo.append((tg, 3, kind, i, n))
+        left = len(plan)
+        for _, step, kind, i, w in sorted(todo):
             win = A("pb" if kind == "P" else "rb", DUM, RAW)
             mine = ("rr%d" if kind == "P" else "pr%d") % t
             n = {"P": "tp", "R": "tr"}[kind]
-            off = A("ct%d" % t, 64 * i, 64 * i + 64)
+            off = A("ct%d" % t, 32 * i, 32 * (i + w))
             if step == 0:
-                tt(A(n, 1024 * i, 1024 * i + 1024), ind(win, off), A(mine), O.is_ge if kind == "P" else O.is_le)
+                tt(A(n, 512 * i, 512 * (i + w)), ind(win, off), A(mine, 0, 512 * w), O.is_ge if kind == "P" else O.is_le)
             elif step == 1:
-                act(A("gp", 1024 * i, 1024 * i + 1024), ind(win, off))
+                act(A("gp", 512 * i, 512 * (i + w)), ind(win, off))
             elif step == 2:
-                for h in (2 * i, 2 * i + 1):
+                for h in range(i, i + w):
                     p = "p%d" % (h % 4)
                     mm(A(p), A("idm"), A("gp", 512 * h, 512 * h + 512), True, False)
                     mm(A(p), A("ngm"), A(mine, 0, 512), False, True)
                     act(A(n, 512 * h, 512 * h + 512), A(p), AF.Relu, bias=1.0, scale=1.0 if kind == "P" else -1.0)
             else:
                 left -= 1
-                squeeze(n, i, left == 0)
+                squeeze(n, i, w, left == 0)
 
     def tree(srcs, op):
         for i in range(len(srcs) - 1):
@@ -322,14 +340,27 @@ def rank_program(g, core, T, topo):
         cp(A("bits"), A("fbt"))
         tt(A("kl", 0, 16), A("kl", 0, 16), A("pen"), O.add)
         tt(A("ke"), ind(A("kl"), A("oke")), A("dg"), O.mult)
-        for p, cl, r in (("p5", "cll", 10), ("p6", "clr", 13)):
-            mm(A(p, 0, 256), A("idm"), A(cl), True, False)
-            mm(A(p, 0, 256), A("sb2m"), A("bits"), False, False)
+        for p, cl in (("p6", "clr"), ("p5", "cll")): mm(A(p, 0, 256), A("idm"), A(cl), True, False)
+        for p in ("p6", "p5"): mm(A(p, 0, 256), A("sb2m"), A("bits"), False, False)
+        for p, r in (("p6", 13), ("p5", 10)):
             mm(A(p, 0, 256), A("wm", 128 * r, 128 * r + 128), A("ke", 0, 256), False, False)
             mm(A(p, 0, 256), A("wm", 128 * r + 128, 128 * r + 256), A("ke", 256, 512), False, True)
         act(A("fr"), A("p6", 0, 256), scale=c(RS))
         act(A("fev"), A("p5", 0, 256), scale=c(RG0))
-        ts(A("fod"), A("p5", 0, 256), c(RG1), O.mult)
+        act(A("fod"), A("p5", 0, 256), scale=c(RG1))
+        tt(A("bm"), ind(fw, A("nl")), A("dg", 0, 256), O.mult)
+        scan(A("bs"), A("sg1"), A("bm"), 0.0, O.mult, O.add)
+        v3 = A("v3", 48 * t, 48 * t + 48)
+        cp(A("nb3", 0, 16), A("nli"))
+        ts(A("nb3", 16, 32), A("bs", 15, 256, 16), float(DUM), O.add)
+        cp(A("nb3", 32, 48), A("bs", 15, 256, 16))
+        tt(A("d3"), A("nb3"), v3, O.subtract)
+        ts(A("ask"), A("mk"), c(LIM), O.is_lt)
+        tt(A("bc"), A("d3", 32, 48), A("has"), O.mult)
+        tt(A("bc"), A("bc"), A("v3", 48 * t + 32, 48 * t + 48), O.add)
+        for i in range(3): tt(A("d3", 16 * i, 16 * i + 16), A("d3", 16 * i, 16 * i + 16), A("ask"), O.mult)
+        cp(A("bcu"), A("bc"))
+        if t + 1 < RO: list_b(t + 1)
         seen = {"V": 0, "S": 0}
         for a in range(16):
             gr, h, who = a // 2, a % 2, PAIRS[a]
@@ -339,18 +370,6 @@ def rank_program(g, core, T, topo):
             mm(A(p, 0, 256), A("fod" if gr % 2 else "fev", 128 * h, 128 * h + 128, p0=lo, p1=lo + 32), A("fr", p0=lo, p1=lo + 32), True, True)
             if who == "V": reduce(A("mx", a, a + 1), A(p, 0, 256), O.max)
             else: act(A("junk"), A(p, 0, 256), AF.Relu, bias=-B10, acc=A("mx", a, a + 1))
-        tt(A("bm"), ind(fw, A("nl")), A("dg", 0, 256), O.mult)
-        scan(A("bs"), A("sg1"), A("bm"), 0.0, O.mult, O.add)
-        v3 = A("v3", 48 * t, 48 * t + 48)
-        cp(A("nb3", 0, 16), A("nli"))
-        ts(A("nb3", 16, 32), A("bs", 15, 256, 16), float(DUM), O.add)
-        cp(A("nb3", 32, 48), A("bs", 15, 256, 16))
-        tt(A("d3"), A("nb3"), v3, O.subtract)
-        tt(A("bc"), A("d3", 32, 48), A("has"), O.mult)
-        tt(A("bc"), A("bc"), A("v3", 48 * t + 32, 48 * t + 48), O.add)
-        ts(A("ask"), A("mk"), c(LIM), O.is_lt)
-        for i in range(3): tt(A("d3", 16 * i, 16 * i + 16), A("d3", 16 * i, 16 * i + 16), A("ask"), O.mult)
-        cp(A("bcu"), A("bc"))
         tt(A("we"), ind(A("mx"), A("omx")), A("thr"), O.is_le)
         for h in range(2): mm(A("p7", 0, 48), A("we", 128 * h, 128 * h + 128), A("rq", 48 * h, 48 * h + 48), h == 0, h == 1)
         tt(A("t3"), A("p7", 0, 48), A("d3"), O.mult)
@@ -408,7 +427,6 @@ def rank_program(g, core, T, topo):
         xr, u = A("xb", RAW + t, RAW + V, 4), t + 1
         scat(A("xb", 0, GH), sc, xr)
         selfmark("xb", t, xr, "p0", "idm", O.min)
-        pwin(t)
         f_changes(t)
         tt(A("xb", DUM + u, GH, 4), A("xb", DUM + u, GH, 4), A("p3", 0, 256), O.max)
 
@@ -416,11 +434,11 @@ def rank_program(g, core, T, topo):
         for m in range(16): mm(A("p6", 0, 32), A("em", 128 * m, 128 * m + 128), A("fl", DUM + m, DUM + G5, 16), m == 0, m == 15)
 
     def f_changes(t):
-        cp(A("fls"), A("p6", 0, 32)); cp(A("fli"), A("fls"))
+        cp(A("fli"), A("p6", 0, 32))
         tt(A("dp"), A("pn%d" % t, 0, 128), A("pr%d" % t, 0, 128), O.not_equal)
-        ts(A("flt"), A("fls"), float(G5), O.is_lt)
+        ts(A("flt"), A("p6", 0, 32), float(G5), O.is_lt)
         ts(A("fli"), A("fli"), 3, O.bitwise_and)
-        tt(A("dfl"), A("fls"), A("fvs"), O.subtract)
+        tt(A("dfl"), A("p6", 0, 32), A("fvs"), O.subtract)
         ts(A("chf"), A("fli"), float(t), O.is_equal, c(NRS + t), O.mult)
         tt(A("dfl"), A("dfl"), A("flt"), O.mult)
         mm(A("p7", 128, 160), A("idm"), A("chf"), True, False)
@@ -474,7 +492,7 @@ def rank_program(g, core, T, topo):
     def ghosts(t):
         arrive("azA%d" % t, 2, [A("lz%d" % t, 0, 32)]); arrive("azB%d" % t, 2, [A("lz%d" % t, 32, 64)])
         for s in "ab":
-            act(A("rw" + s, G5 + t, 2 * G5, 4), A("lr%s%d" % (s, t)))
+            cp(A("rw" + s, G5 + t, 2 * G5, 4), A("lr%s%d" % (s, t)))
             act(A("pw" + s, G5 + t, 2 * G5, 4), A("lp%s%d" % (s, t)))
         cp(A("zi"), A("lz%d" % t))
         ts(A("ei"), A("zi"), 512, O.bitwise_and)
@@ -490,10 +508,14 @@ def rank_program(g, core, T, topo):
             cp(A("rb", *w), ind(A("rv" + s), A("fu", 32 * i, 32 * i + 32)))
 
     turn_a(0)
+    tables()
+    turn_v(0)
+    turn_s(0)
     fill(A("xb", DUM, GH, 4), PEN)
-    turn_b(0)
-    turn_a(1); turn_b(1)
+    list_b(0)
+    turn_a(1)
     copies(0, cp)
+    turn_v(1)
     iota(A("ik"), [[1, 8], [0, 16]])
     ts(A("b8"), A("ik"), c(PF), O.is_equal)
     cp(A("thf", 0, 1, p1=8), A("thi", 0, 1, p1=8))
@@ -503,7 +525,7 @@ def rank_program(g, core, T, topo):
     for i in range(4): x_gather(0, i)
     distances(0)
     iota(A("ib"), [[0, 16], [1, 16]])
-    iota(A("ic"), [[1, 256]])
+    iotf(A("ic"), [[1, 256]])
     iota(A("ih", 0, 16), [[1, 2], [2, 8]]); iota(A("ih", 16, 48), [[1, 32]])
     iota(A("ij", 0, 16), [[0, 16]], 0, 1); iota(A("ij", 16, 32), [[16, 16]], 0, 1)
     iotf(A("vi"), [[1, DUM + V]], -DUM); iotf(A("fl"), [[1, DUM + V]], -DUM); iotf(A("nv"), [[-1, DUM + V]], DUM)
@@ -513,8 +535,6 @@ def rank_program(g, core, T, topo):
     ts(A("dg", 0, 256), A("ib"), c(ROW), O.is_equal); ts(A("dg", 256, 512), A("ib"), c(ROW), O.is_equal)
     cp(A("oke"), A("ih", 16, 48)); cp(A("omx"), A("ih", 0, 16))
     ts(A("oq"), A("ij", 0, 16), c(NG), O.add)
-    ts(A("cll"), A("ic"), c(M12), O.mult, c(C1L), O.add)
-    ts(A("clr"), A("ic"), c(M15), O.mult, c(C1R), O.add)
     for a in range(16):
         o = 128 * (a % 2) + 16 * (a // 2)
         if a == 0: ts(A("thr"), A("dg", 0, 256), 1e9 + 0.5, O.mult, -1e9, O.add)
@@ -550,13 +570,17 @@ def rank_program(g, core, T, topo):
     for t in range(RO):
         last = t == RO - 1
         tests(t)
+        if t == 0: row_tables()
         c_flags()
-        if not last: copies(t + 1, act)
+        if not last:
+            turn_s(t + 1)
+            copies(t + 1, act)
         if t == 0: border()
         partner(t)
         merge(t)
         if last:
-            succ_gather(SUCC)
+            succ_gather(SUCC[:3])
+            for a, b in SUCC[3:]: cp(A("sg", a, b), ind(A("rb", DUM, RAW), A("so", a // 16, b // 16)))
         else:
             scat(A("fl", 0, DUM + V), sc, A("vi", DUM + t, DUM + V, 4))
             if t + 2 < RO: turn_a(t + 2)
@@ -567,7 +591,6 @@ def rank_program(g, core, T, topo):
             block("p", t)
             f_list(t)
         xmerge(t)
-        if t == 0: cp(A("cb"), A("ci"))
         if last:
             dma("D", T.yx[:], RWb("xb")["ap"], [RWb("xb")], [])
             c_update(t)
@@ -577,14 +600,16 @@ def rank_program(g, core, T, topo):
             dma("D", T.yr[:], RWb("rb")["ap"], [RWb("rb")], [])
             continue
         windows(t)
-        if t + 2 < RO: turn_b(t + 2)
         for i in range(4): x_gather(t + 1, i)
         succ_min(t)
         block("r", t)
         publish(t)
+        pwin(t)
         rwin(t)
         distances(t + 1)
+        if t == 0: cp(A("cb"), A("ci"))
         c_update(t)
+        if t + 2 < RO: turn_v(t + 2)
         ghosts(t)
         count(t)
     for i in range(free["ls"]):

from concourse.bass import DstId, RemoteDMATransfer
from concourse.mybir import AluOpType, AxisListType, ActivationFunctionType as AF

V, G5, RO, CAP = 1024, 512, 4, 96
DUM, GH, RAW, WID = 256, 1280, 2304, 3328
PEN = 16384.0
B10 = 10.0 * 2 ** 20
TESTS = (("P", 0, 2, "V"), ("P", 2, 2, "V"), ("P", 4, 2, "V"), ("P", 6, 2, "V"), ("R", 0, 2, "V"), ("R", 2, 1, "V"), ("R", 3, 1, "S"), ("R", 4, 2, "S"), ("R", 6, 2, "S"))
TESTS0 = tuple((k, i, n, "S" if (k, i) == ("R", 6) else "V") for k, i, n, _ in TESTS)
SUCC = ((0, 1024), (1024, 2048), (2048, 3072), (3072, 4096))
PAIRS = "SVSVSVSVSVSVSVSV"

SCRATCH, PLACE = {}, {}
SIZE = {"bfloat16": 2, "uint16": 2, "float32": 4, "int32": 4}


def _b(names, cols, dtype, where="sbuf"):
    for name in names.split():
        if where == "sbuf" and cols <= 512:
            pool = "pool_" + dtype
            at = SCRATCH.get(pool, (where, [128, 0], dtype))[1][1]
            step = 32 // SIZE[dtype]
            SCRATCH[pool] = (where, [128, at + -(-cols // step) * step], dtype)
            PLACE[name] = (pool, at, cols)
        else:
            SCRATCH[name] = (where, [128, cols], dtype)
            PLACE[name] = (name, 0, cols)


_b("xb rb pb", WID, "bfloat16")
_b("fl vi nv", DUM + V, "float32"); _b("idf", 128, "float32")
_b("ci si", V, "int32")
_b("cb sb", V, "float32")
for _t in range(RO):
    _b("rr%d pr%d" % (_t, _t), 1024, "bfloat16")
    _b("ct%d" % _t, 256, "uint16"); _b("ca%d" % _t, 256, "float32")
    _b("xa%d rn%d pn%d" % (_t, _t, _t), 256, "bfloat16"); _b("z%d" % _t, 32, "uint16")
    _b("lra%d lrb%d lpa%d lpb%d" % (_t, _t, _t, _t), 128, "bfloat16")
    _b("lz%d" % _t, 64, "uint16")
_b("xg ad tp tr sg sc gp", 4096, "bfloat16")
_b("rwa rwb pwa pwb", 1024, "bfloat16")
_b("rva rvb pva pvb", 512, "bfloat16")
_b("wm", 2048, "bfloat16"); _b("em", 2048, "float32")
_b("idm ngm bom ltm sb2m onm", 128, "bfloat16"); _b("b8", 128, "float32")
_b("sc10 sc13 sw " + " ".join("se%d" % r for r in range(10, 16)), 1, "float32"); _b("ic", 256, "float32")
_b("ia ib", 256, "int32"); _b("id_ ie ig ih ij ik in_", 128, "int32"); _b("iq", 1024, "int32")
_b("pc", 8, "int32"); _b("cc", 48, "float32"); _b("g8", 8, "bfloat16"); _b("lh", 128, "bfloat16"); _b("lw", 16, "float32")
_b("dg", 512, "bfloat16"); _b("thr sg1", 256, "float32"); _b("smx", 1024, "bfloat16")
_b("kc cll clr", 256, "bfloat16"); _b("rq", 96, "bfloat16"); _b("one", 32, "float32")
_b("o2 ofin oq omx", 16, "uint16"); _b("oke", 32, "uint16")
_b("in12 tr12", 512, "float32")
_b("key", 256, "int32"); _b("k8", 128, "int32"); _b("k4", 64, "int32"); _b("k2", 32, "int32"); _b("mk", 16, "int32")
_b("eq prd", 256, "float32"); _b("s8", 128, "float32"); _b("s4", 64, "float32"); _b("s2", 32, "float32")
_b("s1 has ask nli bc pen", 16, "float32"); _b("nl bcu", 16, "uint16"); _b("fsh fbt", 256, "int32")
_b("bits fev fod fr junk we os", 256, "bfloat16"); _b("bm bs cd od sx sev", 256, "float32"); _b("kl", 32, "int32"); _b("ke", 512, "bfloat16")
_b("mx", 16, "float32"); _b("nb3 d3 t3", 48, "float32"); _b("l3", 48, "uint16"); _b("v3", 192, "float32"); _b("so", 256, "uint16")
_b("xs xh", 256, "int32"); _b("r2 nsm0 nsm1", 256, "bfloat16")
_b("wn", 16, "bfloat16"); _b("mt", 2, "float32"); _b("mi", 2, "int32"); _b("thi", 8, "int32"); _b("thf", 8, "float32")
_b("dr dp", 128, "bfloat16")
_b("fvs e5 flt dfl c96 go ge gf zf", 32, "float32"); _b("fli", 32, "int32"); _b("chf ch scq", 32, "bfloat16")
_b("zi fi ei jl", 64, "int32"); _b("fu eu", 64, "uint16")
_b("p0 p1 p2 p3 p4 p5 p6 p7", 512, "float32", "psum")
SEMAPHORES = ["qV", "qS", "qP", "qG", "inA", "inB"] + ["d%d" % i for i in range(24)] + ["ls%d" % i for i in range(12)] + \
    ["%s%s%d" % (a, s, t) for a in ("ar", "ap", "az") for s in "AB" for t in range(RO - 1)]


def rank_program(g, core, T, topo):
    rank = T.rank_of(core)
    if rank is None:
        return
    O = AluOpType
    queues = {"V": g.vector, "S": g.scalar, "P": g.tensor, "G": g, "D": g.sync}
    cnt = {"qV": 0, "qS": 0, "qP": 0, "qG": 0}
    know = {q: {} for q in queues}
    snap, hist, free = {}, {}, {"d": 0, "ls": 0}

    def A(name, a=None, b=None, s=1, p0=0, p1=128):
        buf, at, cols = PLACE[name]
        t = T[buf]
        a = 0 if a is None else a
        b = cols if b is None else b
        return {"n": name, "a": a, "b": b, "s": s, "ap": t[p0:p1, at + a:at + b:s] if s != 1 else t[p0:p1, at + a:at + b]}

    def wait(q, sem, val):
        if know[q].get(sem, 0) < val:
            queues[q].wait_ge(T.sem[sem], val)
            for k, v in snap.get((sem, val), {}).items():
                if know[q].get(k, 0) < v: know[q][k] = v
            know[q][sem] = val

    def deps(q, reads, writes):
        need = {}
        for acc, w in [(r, False) for r in reads] + [(r, True) for r in writes]:
            ps = SCRATCH[PLACE[acc["n"]][0]][0] == "psum"
            for e in hist.get(acc["n"], ()):
                if e[3] == q and ps and q == "P": continue
                if (w or e[2] or (ps and e[3] != q)) and (ps or (acc["a"] < e[1] and e[0] < acc["b"])):
                    if need.get(e[4], 0) < e[5]: need[e[4]] = e[5]
        for s in sorted(need): wait(q, s, need[s])

    def note(q, sem, val, reads, writes):
        snap[(sem, val)] = dict(know[q])
        for acc, w in [(r, False) for r in reads] + [(r, True) for r in writes]:
            h = hist.setdefault(acc["n"], [])
            if w and acc["s"] == 1:
                h[:] = [e for e in h if not (acc["a"] <= e[0] and e[1] <= acc["b"])]
            else:
                h[:] = [e for e in h if not (e[4] == sem and e[2] == w and e[0] == acc["a"] and e[1] == acc["b"])]
            h.append((acc["a"], acc["b"], w, q, sem, val))

    def run(q, fn, writes, reads):
        deps(q, reads, writes)
        s = "q" + q
        cnt[s] += 1
        fn().then_inc(T.sem[s], 1)
        note(q, s, cnt[s], reads, writes)

    def dma(q, out, in_, reads, writes):
        deps(q, reads, writes)
        s = "d%d" % free["d"]; free["d"] += 1
        queues[q].dma_start(out, in_).then_inc(T.sem[s], 16)
        note(q, s, 16, reads, writes)

    def ind(win, off): return {"ap": win["ap"].indirect(off["ap"]), "w": win, "o": off}
    def rd(x): return [x["w"], x["o"]] if "w" in x else [x]
    def cp(out, in_): run("V", lambda: g.vector.tensor_copy(out["ap"], in_["ap"]), [out], rd(in_))
    def scat(win, off, in_): run("V", lambda: g.vector.tensor_copy(win["ap"].indirect(off["ap"]), in_["ap"]), [win], [off, in_])
    def tt(out, a, b, op): run("V", lambda: g.vector.tensor_tensor(out["ap"], a["ap"], b["ap"], op), [out], rd(a) + [b])
    def ts(out, a, s1, op0, s2=None, op1=None):
        r = rd(a) + [s for s in (s1, s2) if isinstance(s, dict)]
        v1 = s1["ap"] if isinstance(s1, dict) else s1
        v2 = s2["ap"] if isinstance(s2, dict) else s2
        if op1 is None: run("V", lambda: g.vector.tensor_scalar(out["ap"], a["ap"], v1, None, op0), [out], r)
        else: run("V", lambda: g.vector.tensor_scalar(out["ap"], a["ap"], v1, v2, op0, op1), [out], r)
    def scan(out, d0, d1, init, op0, op1): run("V", lambda: g.vector.tensor_tensor_scan(out["ap"], d0["ap"], d1["ap"], init, op0, op1), [out], [d0, d1])
    def fill(out, v): run("V", lambda: g.vector.memset(out["ap"], v), [out], [])
    def reduce(out, in_, op): run("V", lambda: g.vector.tensor_reduce(out["ap"], in_["ap"], AxisListType.X, op), [out], [in_])
    def act(out, in_, func=AF.Copy, bias=0.0, scale=1.0, acc=None):
        r = rd(in_) + [k for k in (bias, scale) if isinstance(k, dict)]
        sc = scale["ap"] if isinstance(scale, dict) else scale
        bi = bias["ap"] if isinstance(bias, dict) else bias
        if acc is None: run("S", lambda: g.scalar.activation(out["ap"], in_["ap"], func, bias=bi, scale=sc), [out], r)
        else: run("S", lambda: g.scalar.activation(out["ap"], in_["ap"], func, bias=bias, scale=sc, accum_out=acc["ap"]), [out, acc], r)
    def mm(out, l, r, start, stop): run("P", lambda: g.tensor.matmul(out["ap"], l["ap"], r["ap"], start, stop), [out], [l, r])
    def iota(out, pat, base=0, cm=0): run("G", lambda: g.iota(out["ap"], pat, base, cm), [out], [])
    def iotf(out, pat, base=0, cm=0): run("G", lambda: g.iota(out["ap"], pat, base, cm, allow_small_or_imprecise_dtypes=True), [out], [])

    nxt, prv = T.cores[(rank + 1) % 8], T.cores[(rank - 1) % 8]
    far = [d for d in (nxt, prv) if topo.chip(d) != topo.chip(core)]
    eng = {}
    for d in (nxt, prv):
        e = topo.engines(core, d)
        if d not in far: e = [i for i in e if not far or i not in topo.engines(core, far[0])] or e
        elif len(far) == 2: e = e[:len(e) // 2] if d == far[0] else e[len(e) // 2:]
        eng[d] = e

    def send(pairs, sems, n):
        s = "ls%d" % free["ls"]; free["ls"] += 1
        deps("G", [p[0] for p in pairs], [])
        tr = []
        for side, d in (("A", prv), ("B", nxt)):
            rid, pid, _ = topo.addr(d)
            for i, p in enumerate(pairs):
                tr.append(RemoteDMATransfer(dst_ids=[DstId(rid=rid, pnc=pid)], dma_engine_mask=sum(1 << e for e in eng[d][i * n:i * n + n]),
                                            remote_sem=T.sem[sems[i] % side], src=p[0]["ap"], dst=p[1 if side == "A" else 2]["ap"]))
        g.remote_dma_fused(tr, local_sem=T.sem[s])
        note("G", s, n * len(tr), [p[0] for p in pairs], [])

    def arrive(sem, val, writes):
        snap[(sem, val)] = {}
        for w in writes: hist.setdefault(w["n"], []).append((w["a"], w["b"], True, "R", sem, val))

    RWb = lambda n: A(n, RAW, RAW + V)
    own = lambda n: A(n, DUM, GH)
    gA, gB = (GH, GH + G5), (GH + G5, GH + 2 * G5)
    dma("D", RWb("rb")["ap"], T.reach[:], [], [RWb("rb")])
    dma("S", RWb("pb")["ap"], T.past[:], [], [RWb("pb")])
    dma("D", A("ci")["ap"], T.cand[:], [], [A("ci")])
    dma("S", own("xb")["ap"], T.x[:], [], [own("xb")])
    dma("D", RWb("xb")["ap"], T.x[:], [], [RWb("xb")])
    dma("D", own("rb")["ap"], T.reach[:], [], [own("rb")])
    dma("D", own("pb")["ap"], T.past[:], [], [own("pb")])
    dma("D", A("si")["ap"], T.succ[:], [], [A("si")])
    dma("D", A("thi", 0, 1, p1=8)["ap"], T.th[:], [], [A("thi")])
    c = lambda i: A("cc", i, i + 1)
    ROW, P16, PF, ODD, SCL, RS, RG0, RG1, C1L, C1R, M12, M15, TH16, NG, LIM, EVR, W0, W1, W2, W3, W4 = range(21)
    NRS, PM = 24, 28
    rw, pp = A("pc", 1, 2), A("pc", 0, 1)
    iota(pp, [[0, 1]], 0, 1)
    iota(A("id_", 0, 16), [[32, 8], [-16, 2]], 16, 1)
    iota(A("id_", 16, 32), [[1, 16]])
    iota(A("ie"), [[1, 128]])
    iota(A("ig", 0, 8), [[1, 8]])
    iota(A("ia"), [[1, 16], [0, 16]])
    iotf(A("xb", GH, RAW), [[0, RAW - GH]], int(PEN))
    send([(A("rb", RAW, RAW + G5), A("rb", *gA), A("rb", *gB)), (A("pb", RAW, RAW + G5), A("pb", *gA), A("pb", *gB))], ["in%s", "in%s"], 4)
    for n in ("rb", "pb"):
        arrive("inA", 8, [A(n, *gA)]); arrive("inB", 8, [A(n, *gB)])
    ts(rw, pp, 15, O.bitwise_and)
    ts(A("pc", 2, 3), pp, 4, O.arith_shift_right)
    ts(A("pc", 3, 4), pp, 4, O.arith_shift_right, 1, O.bitwise_and)
    ts(A("pc", 4, 5), rw, 1, O.arith_shift_right)
    ts(A("pc", 5, 6), rw, 1, O.bitwise_and)
    cp(c(ROW), rw); cp(c(P16), A("pc", 2, 3)); cp(c(PF), pp); cp(c(RG1), A("pc", 3, 4)); cp(c(W0), A("pc", 4, 5)); cp(c(ODD), A("pc", 5, 6))
    ts(c(RG0), c(RG1), -1.0, O.mult, 1.0, O.add)
    ts(c(EVR), c(ODD), -1.0, O.mult, 1.0, O.add)
    ts(c(NG), c(P16), -16.0, O.mult)
    ts(A("o2"), A("id_", 0, 16), c(NG), O.add)
    tt(c(W1), c(ODD), c(RG1), O.not_equal)
    ts(c(W2), c(W0), 32.0, O.mult)
    ts(c(W1), c(W1), 256.0, O.mult, c(W2), O.add)
    ts(c(W2), c(RG1), 16.0, O.mult, c(W1), O.add)
    ts(A("ofin"), A("id_", 16, 32), c(W2), O.add)
    def tables():
        ts(A("g8"), A("ig", 0, 8), c(P16), O.is_equal)
        fill(A("wm"), 0.0)
        for m in range(16): act(A("wm", 128 * m + m, 128 * m + 128, 16), A("g8"))
        ts(A("idm"), A("ie"), c(PF), O.is_equal)
        ts(A("ngm"), A("idm"), -1.0, O.mult)
        ts(A("kc"), A("ia"), 2.0 ** -23, O.mult)
        fill(A("smx"), 0.0); fill(A("smx", 0, 1024, 16), 255.0)
        fill(A("sg1"), 1.0); fill(A("sg1", 0, 256, 16), 0.0)
        fill(A("nsm0"), 0.0)

    def row_tables():
        fill(c(SCL), 1.0)
        for b in range(4):
            ts(A("pc", 7, 8), rw, b, O.arith_shift_right, 1, O.bitwise_and)
            ts(c(W3), A("pc", 7, 8), 2.0 ** -(2 ** b) - 1.0, O.mult, 1.0, O.add)
            tt(c(SCL), c(SCL), c(W3), O.mult)
        eq, lt = {}, {}
        for lim in (10, 13):
            lt[lim] = A("sc%d" % lim)
            act(A("sw"), c(ROW), AF.Sign, bias=lim - 0.5, scale=-1.0)
            act(lt[lim], A("sw"), AF.Relu)
        for r in (10, 11, 12, 13, 14, 15):
            eq[r] = A("se%d" % r)
            act(A("sw"), c(ROW), AF.Abs, bias=-float(r))
            act(eq[r], A("sw"), AF.Relu, bias=1.0, scale=-1.0)

        def total(i, parts):
            for n, (m, v) in enumerate(parts):
                act(c(i), m, AF.Identity, bias=c(i) if n else 0.0, scale=float(v))
        total(RS, [(lt[10], 2 ** 20), (eq[10], 2 ** 14), (eq[11], 2 ** 8), (eq[12], 1), (eq[13], -2 ** 14), (eq[14], -2 ** 8), (eq[15], -1)])
        total(C1L, [(lt[10], -1), (eq[13], 1), (eq[14], 1), (eq[15], 1)])
        total(C1R, [(lt[10], -2), (lt[13], 1)])
        act(c(W4), lt[10], scale=2.0)
        act(A("cll"), A("ic"), AF.Identity, bias=c(C1L), scale=eq[12])
        act(A("clr"), A("ic"), AF.Identity, bias=c(C1R), scale=eq[15])
        act(A("sb2m"), A("idm"), scale=c(W4))
        act(A("idf"), A("idm"))

    def turn_a(t):
        cp(A("in12", 0, 256), A("ci", t, V, 4))
        act(A("in12", 256, 512), ind(A("in12", 0, 256), A("o2")))

    def turn_v(t): run("V", lambda: g.vector.transpose(A("tr12")["ap"], A("in12")["ap"]), [A("tr12")], [A("in12")])

    def turn_s(t): act(A("ca%d" % t), ind(A("tr12"), A("ofin")))

    def list_b(t): cp(A("ct%d" % t), A("ca%d" % t))

    def copies(t, f):
        f(A("xa%d" % t), A("xb", RAW + t, RAW + V, 4))
        for n in ("r", "p"):
            for i in range(4): f(A("%sr%d" % (n, t), 256 * i, 256 * i + 256), A(n + "b", RAW + t, RAW + V, 4))

    def squeeze(n, i, w, last):
        for m in range(16):
            mm(A("p4", 32 * i, 32 * (i + w)), A("wm", 128 * m, 128 * m + 128), A(n, 512 * i + m, 512 * (i + w), 16), False, last and m == 15)

    def x_gather(t, i): act(A("xg", 1024 * i, 1024 * i + 1024), ind(A("xb", DUM, RAW), A("ct%d" % t, 64 * i, 64 * i + 64)))

    def x_sub(t, i):
        for h in (2 * i, 2 * i + 1):
            p = "p%d" % (h % 4)
            mm(A(p), A("idm"), A("xg", 512 * h, 512 * h + 512), True, False)
            mm(A(p, 0, 256), A("ngm"), A("xa%d" % t), False, False)
            mm(A(p, 256, 512), A("ngm"), A("xa%d" % t), False, True)

    def distances(t):
        mm(A("p4", 0, 256), A("idm"), A("kc"), True, False)
        x_sub(t, 0)
        for i in range(4):
            if i < 3: x_sub(t, i + 1)
            for h in (2 * i, 2 * i + 1): act(A("ad", 512 * h, 512 * h + 512), A("p%d" % (h % 4)), AF.Abs, scale=2.0 ** -19)
            squeeze("ad", 2 * i, 2, False)

    def tests(t):
        todo, tv, tg = [], 0.0, 0.0
        plan = TESTS if t else TESTS0
        for kind, i, n, who in plan:
            if who == "V":
                todo.append((tv, 0, kind, i, n)); tv += 0.8 * n; todo.append((tv, 3, kind, i, n))
            else:
                todo.append((tg, 1, kind, i, n)); tg += 0.8 * n
        for kind, i, n, who in plan:
            if who == "S":
                todo.append((tg, 2, kind, i, n)); tg += 0.65 * n; todo.append((tg, 3, kind, i, n))
        left = len(plan)
        for _, step, kind, i, w in sorted(todo):
            win = A("pb" if kind == "P" else "rb", DUM, RAW)
            mine = ("rr%d" if kind == "P" else "pr%d") % t
            n = {"P": "tp", "R": "tr"}[kind]
            off = A("ct%d" % t, 32 * i, 32 * (i + w))
            if step == 0:
                tt(A(n, 512 * i, 512 * (i + w)), ind(win, off), A(mine, 0, 512 * w), O.is_ge if kind == "P" else O.is_le)
            elif step == 1:
                act(A("gp", 512 * i, 512 * (i + w)), ind(win, off))
            elif step == 2:
                for h in range(i, i + w):
                    p = "p%d" % (h % 4)
                    mm(A(p), A("idm"), A("gp", 512 * h, 512 * h + 512), True, False)
                    mm(A(p), A("ngm"), A(mine, 0, 512), False, True)
                    act(A(n, 512 * h, 512 * h + 512), A(p), AF.Relu, bias=1.0, scale=1.0 if kind == "P" else -1.0)
            else:
                left -= 1
                squeeze(n, i, w, left == 0)

    def tree(srcs, op):
        for i in range(len(srcs) - 1):
            w = 128 >> i
            tt(A(srcs[i + 1]), A(srcs[i], 0, w), A(srcs[i], w, 2 * w), op)

    def partner(t):
        ts(A("key"), A("p4", 0, 256), 2.0 ** 23, O.mult, 2.0 ** 22, O.min)
        tree(("key", "k8", "k4", "k2", "mk"), O.min)
        tt(A("eq"), ind(A("mk"), A("oq")), A("key"), O.is_equal)
        tt(A("prd"), A("eq"), A("ca%d" % t), O.mult)
        ts(A("has"), A("mk"), 65536.0, O.is_lt)
        tree(("prd", "s8", "s4", "s2", "s1"), O.add)
        tt(A("nli"), A("s1"), A("has"), O.mult)
        cp(A("nl"), A("nli"))
        fw = A("fl", DUM, DUM + V)
        ts(A("fsh"), ind(fw, A("nl")), c(SCL), O.mult, -0.5 + 2.0 ** -11, O.add)
        ts(A("kl", 0, 16), A("mk"), 10, O.arith_shift_right, 63, O.bitwise_and)
        ts(A("fbt"), A("fsh"), 1, O.bitwise_and)
        ts(A("pen"), A("mk"), c(LIM), O.is_ge, 128.0, O.mult)
        ts(A("kl", 16, 32), A("mk"), 4, O.arith_shift_right, 63, O.bitwise_and)
        cp(A("bits"), A("fbt"))
        tt(A("kl", 0, 16), A("kl", 0, 16), A("pen"), O.add)
        tt(A("ke"), ind(A("kl"), A("oke")), A("dg"), O.mult)
        for p, cl in (("p6", "clr"), ("p5", "cll")): mm(A(p, 0, 256), A("idm"), A(cl), True, False)
        for p in ("p6", "p5"): mm(A(p, 0, 256), A("sb2m"), A("bits"), False, False)
        for p, r in (("p6", 13), ("p5", 10)):
            mm(A(p, 0, 256), A("wm", 128 * r, 128 * r + 128), A("ke", 0, 256), False, False)
            mm(A(p, 0, 256), A("wm", 128 * r + 128, 128 * r + 256), A("ke", 256, 512), False, True)
        act(A("fr"), A("p6", 0, 256), scale=c(RS))
        act(A("fev"), A("p5", 0, 256), scale=c(RG0))
        act(A("fod"), A("p5", 0, 256), scale=c(RG1))
        tt(A("bm"), ind(fw, A("nl")), A("dg", 0, 256), O.mult)
        scan(A("bs"), A("sg1"), A("bm"), 0.0, O.mult, O.add)
        v3 = A("v3", 48 * t, 48 * t + 48)
        cp(A("nb3", 0, 16), A("nli"))
        ts(A("nb3", 16, 32), A("bs", 15, 256, 16), float(DUM), O.add)
        cp(A("nb3", 32, 48), A("bs", 15, 256, 16))
        tt(A("d3"), A("nb3"), v3, O.subtract)
        ts(A("ask"), A("mk"), c(LIM), O.is_lt)
        tt(A("bc"), A("d3", 32, 48), A("has"), O.mult)
        tt(A("bc"), A("bc"), A("v3", 48 * t + 32, 48 * t + 48), O.add)
        for i in range(3): tt(A("d3", 16 * i, 16 * i + 16), A("d3", 16 * i, 16 * i + 16), A("ask"), O.mult)
        cp(A("bcu"), A("bc"))
        if t + 1 < RO: list_b(t + 1)
        seen = {"V": 0, "S": 0}
        for a in range(16):
            gr, h, who = a // 2, a % 2, PAIRS[a]
            p = {"V": ("p0", "p2", "p5"), "S": ("p1", "p3", "p6")}[who][seen[who] % 3]
            seen[who] += 1
            lo = 32 * (gr // 2)
            mm(A(p, 0, 256), A("fod" if gr % 2 else "fev", 128 * h, 128 * h + 128, p0=lo, p1=lo + 32), A("fr", p0=lo, p1=lo + 32), True, True)
            if who == "V": reduce(A("mx", a, a + 1), A(p, 0, 256), O.max)
            else: act(A("junk"), A(p, 0, 256), AF.Relu, bias=-B10, acc=A("mx", a, a + 1))
        tt(A("we"), ind(A("mx"), A("omx")), A("thr"), O.is_le)
        for h in range(2): mm(A("p7", 0, 48), A("we", 128 * h, 128 * h + 128), A("rq", 48 * h, 48 * h + 48), h == 0, h == 1)
        tt(A("t3"), A("p7", 0, 48), A("d3"), O.mult)
        tt(A("t3"), A("t3"), v3, O.add)
        cp(A("l3"), A("t3"))

    nl2, sc, sl = A("l3", 0, 16), A("l3", 16, 32), A("l3", 32, 48)

    def selfmark(n, t, new, p, sign, op):
        w = A(n, DUM + t, GH, 4)
        mm(A(p, 0, 256), A("idm"), new, True, False)
        mm(A(p, 0, 256), A(sign), A("nsm%d" % (t % 2)), False, True)
        tt(w, w, A(p, 0, 256), op)

    def merge(t):
        tt(A("r2"), ind(A("rb", DUM, WID), nl2), A("rr%d" % t, 0, 256), O.min)
        ts(A("sx"), ind(A("sb"), sl), c(ODD), O.mult)
        scat(A("rb", 0, GH), sc, A("r2"))
        tt(A("sb", t, V, 4), A("sx"), A("sev"), O.add)
        cp(A("so"), A("sb", t, V, 4))
        selfmark("rb", t, A("r2"), "p1", "idm", O.min)

    def succ_gather(chunks):
        for a, b in chunks: act(A("sg", a, b), ind(A("rb", DUM, RAW), A("so", a // 16, b // 16)))

    def succ_min(t):
        for a, b in SUCC: scan(A("sc", a, b), A("smx", 0, b - a), A("sg", a, b), 255.0, O.max, O.min)
        tt(A("rn%d" % t), A("sc", 15, 4096, 16), A("r2"), O.min)

    def pmerge(t): tt(A("pn%d" % t), ind(A("pb", DUM, WID), nl2), A("pr%d" % t, 0, 256), O.max)

    def xmerge(t):
        tt(A("xs"), ind(A("xb", DUM, WID), nl2), A("xa%d" % t), O.add)
        ts(A("xh"), A("xs"), 1, O.arith_shift_right)
        cp(A("xb", RAW + t, RAW + V, 4), A("xh"))

    def c_flags():
        for k in range(16): mm(A("p5", 0, 256), A("wm", 128 * k, 128 * k + 128), A("tp", 256 * k, 256 * k + 256), k == 0, False)
        for k in range(16): mm(A("p5", 0, 256), A("wm", 128 * k, 128 * k + 128), A("tr", 256 * k, 256 * k + 256), False, k == 15)
        act(A("os"), A("p5", 0, 256), AF.Sign)

    def c_update(t):
        tt(A("cd"), ind(A("cb"), A("bcu")), A("ci", t, V, 4), O.subtract)
        tt(A("od"), A("os"), A("cd"), O.mult)
        tt(A("cb", t, V, 4), A("cb", t, V, 4), A("od"), O.add)

    def marks(u):
        ns = A("nsm%d" % (u % 2))
        mm(A("p2", 0, 256), A("idf"), A("fl", DUM + u, DUM + V, 4), True, False)
        mm(A("p2", 0, 256), A("idf"), A("nv", DUM + u, DUM + V, 4), False, True)
        act(ns, A("p2", 0, 256), AF.Abs, scale=PEN)
        act(A("p3", 0, 256), ns, AF.Relu, bias=PEN, scale=-1.0)

    def windows(t):
        xr, u = A("xb", RAW + t, RAW + V, 4), t + 1
        scat(A("xb", 0, GH), sc, xr)
        selfmark("xb", t, xr, "p0", "idm", O.min)
        f_changes(t)
        tt(A("xb", DUM + u, GH, 4), A("xb", DUM + u, GH, 4), A("p3", 0, 256), O.max)

    def f_list(t):
        for m in range(16): mm(A("p6", 0, 32), A("em", 128 * m, 128 * m + 128), A("fl", DUM + m, DUM + G5, 16), m == 0, m == 15)

    def f_changes(t):
        cp(A("fli"), A("p6", 0, 32))
        tt(A("dp"), A("pn%d" % t, 0, 128), A("pr%d" % t, 0, 128), O.not_equal)
        ts(A("flt"), A("p6", 0, 32), float(G5), O.is_lt)
        ts(A("fli"), A("fli"), 3, O.bitwise_and)
        tt(A("dfl"), A("p6", 0, 32), A("fvs"), O.subtract)
        ts(A("chf"), A("fli"), float(t), O.is_equal, c(NRS + t), O.mult)
        tt(A("dfl"), A("dfl"), A("flt"), O.mult)
        mm(A("p7", 128, 160), A("idm"), A("chf"), True, False)
        changed("dp", t, False)

    def changed(n, t, last):
        for a in range(4):
            m = 4 * a + t
            mm(A("p7", 128, 160), A("wm", 128 * m, 128 * m + 128), A(n, a, 128, 4), False, last and a == 3)

    def publish(t):
        tt(A("dr"), A("rn%d" % t, 0, 128), A("rr%d" % t, 0, 128), O.not_equal)
        changed("dr", t, True)
        ts(A("ch"), A("p7", 128, 160), 0.0, O.is_gt)
        scan(A("scq"), A("one"), A("ch"), 0.0, O.mult, O.add)
        ts(A("c96"), A("ch"), float(CAP + 1), O.mult, -1.0, O.add)
        mm(A("p7", 192, 224), A("ltm"), A("ch"), True, False)
        mm(A("p7", 192, 224), A("bom"), A("scq"), False, True)
        tt(A("go"), A("p7", 192, 224), A("c96"), O.is_le)
        ts(A("ge"), A("go"), c(PM + t), O.mult)
        tt(A("gf"), A("go"), A("dfl"), O.mult)
        tt(A("e5"), A("e5"), A("ge"), O.max)
        tt(A("fvs"), A("fvs"), A("gf"), O.add)
        tt(A("zf"), A("e5"), A("fvs"), O.add)
        cp(A("z%d" % t), A("zf"))
        send([(A("z%d" % t), A("lz%d" % t, 0, 32), A("lz%d" % t, 32, 64))], ["az%%s%d" % t], 2)

    def pwin(t):
        scat(A("pb", 0, GH), sc, A("pn%d" % t))
        selfmark("pb", t, A("pn%d" % t), "p2", "ngm", O.max)

    def rwin(t):
        scat(A("rb", 0, GH), sc, A("rn%d" % t))
        selfmark("rb", t, A("rn%d" % t), "p1", "idm", O.min)
        ts(A("sev"), A("si", t + 1, V, 4), c(EVR), O.mult)
        act(A("rb", RAW + t, RAW + V, 4), A("rn%d" % t))

    def count(t):
        tt(A("wn"), A("p7", 0, 16), A("ask"), O.mult)
        mm(A("p7", 256, 272), A("onm"), A("wn"), True, True)
        reduce(A("mt", 0, 1), A("p7", 256, 272), O.add)
        cp(A("mi", 0, 1), A("mt", 0, 1))
        ts(A("mi", 1, 2), A("mi", 0, 1), 31, O.bitwise_and)
        ts(c(LIM), A("mi", 1, 2), 16.0, O.mult, c(TH16), O.add)

    def block(kind, t):
        n = "%sn%d" % (kind, t)
        send([(A(n, 0, 128), A("l%sa%d" % (kind, t)), A("l%sb%d" % (kind, t)))], ["a%s%%s%d" % (kind, t)], 2)
        for s, S in (("a", "A"), ("b", "B")): arrive("a%s%s%d" % (kind, S, t), 2, [A("l%s%s%d" % (kind, s, t))])

    def ghosts(t):
        arrive("azA%d" % t, 2, [A("lz%d" % t, 0, 32)]); arrive("azB%d" % t, 2, [A("lz%d" % t, 32, 64)])
        for s in "ab":
            cp(A("rw" + s, G5 + t, 2 * G5, 4), A("lr%s%d" % (s, t)))
            act(A("pw" + s, G5 + t, 2 * G5, 4), A("lp%s%d" % (s, t)))
        cp(A("zi"), A("lz%d" % t))
        ts(A("ei"), A("zi"), 512, O.bitwise_and)
        ts(A("fi"), A("zi"), 511, O.bitwise_and)
        tt(A("ei"), A("ei"), A("jl"), O.add)
        cp(A("fu"), A("fi"))
        cp(A("eu"), A("ei"))
        for i, s in enumerate("ab"):
            act(A("pv" + s), ind(A("pw" + s), A("eu", 32 * i, 32 * i + 32)))
            cp(A("rv" + s), ind(A("rw" + s), A("eu", 32 * i, 32 * i + 32)))
        for i, (s, w) in enumerate((("a", gA), ("b", gB))):
            act(A("pb", *w), ind(A("pv" + s), A("fu", 32 * i, 32 * i + 32)))
            cp(A("rb", *w), ind(A("rv" + s), A("fu", 32 * i, 32 * i + 32)))

    turn_a(0)
    tables()
    turn_v(0)
    turn_s(0)
    fill(A("xb", DUM, GH, 4), PEN)
    list_b(0)
    turn_a(1)
    copies(0, cp)
    turn_v(1)
    iota(A("ik"), [[1, 8], [0, 16]])
    ts(A("b8"), A("ik"), c(PF), O.is_equal)
    cp(A("thf", 0, 1, p1=8), A("thi", 0, 1, p1=8))
    mm(A("p7", 0, 1), A("b8", p1=8), A("thf", 0, 1, p1=8), True, True)
    ts(c(TH16), A("p7", 0, 1), 16.0, O.mult)
    cp(c(LIM), c(TH16))
    for i in range(4): x_gather(0, i)
    distances(0)
    iota(A("ib"), [[0, 16], [1, 16]])
    iotf(A("ic"), [[1, 256]])
    iota(A("ih", 0, 16), [[1, 2], [2, 8]]); iota(A("ih", 16, 48), [[1, 32]])
    iota(A("ij", 0, 16), [[0, 16]], 0, 1); iota(A("ij", 16, 32), [[16, 16]], 0, 1)
    iotf(A("vi"), [[1, DUM + V]], -DUM); iotf(A("fl"), [[1, DUM + V]], -DUM); iotf(A("nv"), [[-1, DUM + V]], DUM)
    iota(A("in_", 0, 96), [[-8, 2], [0, 3], [1, 16]])
    iota(A("id_", 32, 96), [[0, 2], [16, 32]], 0, 1)
    iotf(A("em"), [[0, 2048]])
    ts(A("dg", 0, 256), A("ib"), c(ROW), O.is_equal); ts(A("dg", 256, 512), A("ib"), c(ROW), O.is_equal)
    cp(A("oke"), A("ih", 16, 48)); cp(A("omx"), A("ih", 0, 16))
    ts(A("oq"), A("ij", 0, 16), c(NG), O.add)
    for a in range(16):
        o = 128 * (a % 2) + 16 * (a // 2)
        if a == 0: ts(A("thr"), A("dg", 0, 256), 1e9 + 0.5, O.mult, -1e9, O.add)
        if PAIRS[a] == "V": ts(A("thr", o, o + 16), A("dg", 0, 16), 1e9 + B10, O.mult, -1e9, O.add)
    ts(A("rq"), A("in_", 0, 96), c(P16), O.is_equal)
    ts(A("lw"), A("ij", 16, 32), c(NG), O.add)
    for t in range(RO):
        o = 48 * t
        ts(A("v3", o, o + 16), A("lw"), 4.0, O.mult, float(2048 + t), O.add)
        cp(A("v3", o + 16, o + 32), A("lw"))
        ts(A("v3", o + 32, o + 48), A("lw"), 4.0, O.mult, float(t), O.add)
    cp(A("sb"), A("si"))
    ts(A("sev"), A("si", 0, V, 4), c(EVR), O.mult)
    for n in ("r", "p"):
        for s, w in (("a", gA), ("b", gB)):
            for o in (0, G5):
                dma("D", A(n + "w" + s, o, o + G5)["ap"], A(n + "b", *w)["ap"], [A(n + "b", *w)], [A(n + "w" + s, o, o + G5)])

    def border():
        for m in range(16): act(A("em", 128 * m + m, 128 * m + 128, 16), A("idm", m, 128, 16))
        ts(A("bom"), A("ik"), c(P16), O.is_equal)
        ts(A("lh"), A("ie"), c(PF), O.is_lt, -1.0, O.mult)
        tt(A("ltm"), A("lh"), A("bom"), O.mult)
        ts(A("jl"), A("id_", 32, 96), c(NG), O.add)
        cp(A("fvs"), A("jl", 0, 32)); fill(A("e5"), 0.0)
        fill(A("one"), 1.0); fill(A("onm"), 1.0)
        ts(A("pc", 7, 8), rw, 3, O.bitwise_and)
        cp(c(W3), A("pc", 7, 8))
        for t in range(RO - 1):
            ts(c(NRS + t), c(W3), float(t), O.not_equal)
            ts(c(PM + t), c(W3), float(t), O.is_le, 512.0, O.mult)

    for t in range(RO):
        last = t == RO - 1
        tests(t)
        if t == 0: row_tables()
        c_flags()
        if not last:
            turn_s(t + 1)
            copies(t + 1, act)
        if t == 0: border()
        partner(t)
        merge(t)
        if last:
            succ_gather(SUCC[:3])
            for a, b in SUCC[3:]: cp(A("sg", a, b), ind(A("rb", DUM, RAW), A("so", a // 16, b // 16)))
        else:
            scat(A("fl", 0, DUM + V), sc, A("vi", DUM + t, DUM + V, 4))
            if t + 2 < RO: turn_a(t + 2)
            succ_gather(SUCC[:2])
            marks(t + 1)
            succ_gather(SUCC[2:])
            pmerge(t)
            block("p", t)
            f_list(t)
        xmerge(t)
        if last:
            dma("D", T.yx[:], RWb("xb")["ap"], [RWb("xb")], [])
            c_update(t)
            dma("D", T.yc[:], A("cb")["ap"], [A("cb")], [])
            succ_min(t)
            cp(A("rb", RAW + t, RAW + V, 4), A("rn%d" % t))
            dma("D", T.yr[:], RWb("rb")["ap"], [RWb("rb")], [])
            continue
        windows(t)
        for i in range(4): x_gather(t + 1, i)
        succ_min(t)
        block("r", t)
        publish(t)
        pwin(t)
        rwin(t)
        distances(t + 1)
        if t == 0: cp(A("cb"), A("ci"))
        c_update(t)
        if t + 2 < RO: turn_v(t + 2)
        ghosts(t)
        count(t)
    for i in range(free["ls"]):
        for (s, v) in [k for k in snap if k[0] == "ls%d" % i]: wait("G", s, v)
    for s in sorted(cnt): wait("G", s, cnt[s])
    for i in range(free["d"]): wait("D", "d%d" % i, 16)
